import numpy as np
import ml_dtypes


def mxq(x, axis, fmt="e4m3"):
    dtype, down = {"e4m3": (ml_dtypes.float8_e4m3fn, 7), "e5m2": (ml_dtypes.float8_e5m2, 14)}[fmt]
    v = np.moveaxis(np.asarray(x, np.float32).astype(ml_dtypes.bfloat16).astype(np.float64), axis, -1)
    blocks = v.reshape(v.shape[:-1] + (-1, 32))
    amax = np.abs(blocks).max(-1, keepdims=True)
    byte = np.maximum(np.where(amax > 0, np.frexp(amax)[1] - 1 + 127, 0) - down, 1)
    scale = np.exp2(byte - 127.0)
    codes = (blocks / scale).astype(np.float32).astype(dtype).astype(np.float64)
    return np.moveaxis((codes * scale).reshape(v.shape), -1, axis)


WIDE = False


def mx_kscale(k):
    if not WIDE:
        return np.ones(k)
    levels = np.array([10, -10, 5, -5, 0])
    if k % 512:
        return np.exp2(np.random.permutation(np.resize(levels, k // 32))).repeat(32)
    a = np.empty((k // 512, 16))
    for p in range(k // 512):
        a[p, :8] = np.random.permutation(np.resize(levels, 8))
        for g in range(8):
            far = levels[np.abs(levels - a[p, g]) >= 10]
            a[p, g + 8] = far[np.random.randint(len(far))]
    return np.exp2(a.ravel()).repeat(32)


def f64(x):
    return np.asarray(x).astype(np.float64)


def striped(idx):
    return np.tile(idx.reshape(-1, 16).T, (8, 1)).astype(np.uint16)


def unstriped(offs):
    return offs[:16].T.reshape(-1).astype(np.int64)


def pack_weight(w):
    k, n = w.shape
    w = f64(np.asarray(w, np.float32).astype(ml_dtypes.bfloat16)).reshape(k // 32, 32, n)
    amax = np.abs(w).max(1)
    byte = np.clip(np.where(amax > 0, np.frexp(amax)[1] - 1 + 127 - 7, 1), 1, 254)
    scaled = (w * np.exp2(127.0 - byte)[:, None, :]).reshape(k, n).astype(np.float32)
    words = np.ascontiguousarray(scaled.reshape(k // 512, 128, 4, n).transpose(0, 1, 3, 2)).astype(ml_dtypes.float8_e4m3fn).view(np.uint8)
    return words, np.ascontiguousarray(byte.astype(np.uint8).reshape(k // 512, 16, n))


def unpack_weight(words, scales):
    g, p, n, _ = words.shape
    vals = np.ascontiguousarray(words).view(ml_dtypes.float8_e4m3fn).astype(np.float64) * np.repeat(np.exp2(scales.astype(np.float64) - 127.0), 8, axis=1)[..., None]
    return vals.transpose(0, 1, 3, 2).reshape(g * 512, n)


E2M1 = np.array([0.0, 0.5, 1.0, 1.5, 2.0, 3.0, 4.0, 6.0, -0.0, -0.5, -1.0, -1.5, -2.0, -3.0, -4.0, -6.0])


def pack_fp4(w):
    k, n = w.shape
    w = f64(np.asarray(w, np.float32).astype(ml_dtypes.bfloat16)).reshape(k // 32, 32, n)
    amax = np.abs(w).max(1)
    mant, ex = np.frexp(amax / 6.0)
    byte = np.clip(np.where(amax > 0, np.where(mant > 0.5, ex, ex - 1) + 127, 1), 1, 254)
    scaled = (w * np.exp2(127.0 - byte)[:, None, :]).reshape(k, n).astype(np.float32)
    c = np.ascontiguousarray(scaled.reshape(k // 512, 128, 4, n).transpose(0, 1, 3, 2)).astype(ml_dtypes.float4_e2m1fn).view(np.uint8) & 0xF
    words = (c[..., 0::2] | (c[..., 1::2] << 4)).reshape(k // 512, 128, 2 * n)
    return np.ascontiguousarray(words), np.ascontiguousarray(byte.astype(np.uint8).reshape(k // 512, 16, n))


def unpack_fp4(words, scales):
    g, _, n = scales.shape
    words = np.ascontiguousarray(words).reshape(g, 128, n, 2)
    nib = np.empty((g, 128, n, 4), np.uint8)
    nib[..., 0::2] = words & 0xF
    nib[..., 1::2] = words >> 4
    vals = E2M1[nib] * np.repeat(np.exp2(scales.astype(np.float64) - 127.0), 8, axis=1)[..., None]
    return vals.transpose(0, 1, 3, 2).reshape(g * 512, n)


def planes(y):
    n, m = y.shape
    v = y.astype(np.float32).astype(ml_dtypes.bfloat16).astype(np.float64).reshape(n // 32, 32, m)
    top = np.abs(v).max(1)
    byte = np.clip(np.where(top > 0, np.frexp(top)[1] - 1 + 127 - 7, 1), 1, 254)
    codes = (v * np.exp2(127.0 - byte)[:, None, :]).reshape(n, m).astype(np.float32).astype(ml_dtypes.float8_e4m3fn).view(np.uint8)
    words = codes.reshape(n // 512, 128, 4, m).transpose(0, 1, 3, 2)
    return np.ascontiguousarray(words), np.ascontiguousarray(byte.astype(np.uint8).reshape(n // 512, 16, m))


K, T, S, N, H, U = 1024, 2048, 512, 512, 512, 1024


def setup_inputs():
    n = np.random.standard_normal
    s = mx_kscale(K)[:, None]
    u = mx_kscale(H)
    packed_xT = pack_weight(n((K, T)) * s)
    packed_w1 = pack_fp4(n((K, N)) / np.sqrt(K) / s)
    packed_w2 = pack_fp4(n((K, N)) / np.sqrt(K) / s)
    packed_w3 = pack_fp4(n((H, N)) / np.sqrt(H) / u[:, None])
    return {
        "x_words": packed_xT[0],
        "x_scales": packed_xT[1],
        "w1_words": packed_w1[0],
        "w1_scales": packed_w1[1],
        "w2_words": packed_w2[0],
        "w2_scales": packed_w2[1],
        "unit": (np.random.uniform(0.6, 1.4, (H, 1)) * u[:, None]).astype(np.float32),
        "w3_words": packed_w3[0],
        "w3_scales": packed_w3[1],
        "offs": striped(np.random.permutation(T)[:S]),
        "bk": striped(np.random.permutation(np.concatenate([np.arange(S), np.random.randint(0, S, U - S)]))),
        "rw_": striped(np.random.permutation(np.concatenate([np.arange(S), np.random.randint(0, S, U - S)]))),
    }


def reference(x_words, x_scales, w1_words, w1_scales, w2_words, w2_scales, unit, w3_words, w3_scales, offs, bk, rw_):
    xq = unpack_weight(x_words, x_scales)[:, unstriped(offs)]
    y = unpack_fp4(w1_words, w1_scales).T @ xq
    yk = y[:, unstriped(bk)]
    yr = y[:, unstriped(rw_)]
    busy = np.maximum(yk, yr)
    z1 = unpack_fp4(w2_words, w2_scales).T @ xq
    zk = z1[:, unstriped(bk)]
    zr = z1[:, unstriped(rw_)]
    hid = f64(unit) * (busy * zk + zr)
    out_0 = unpack_fp4(w3_words, w3_scales).T @ mxq(hid, 0, "e4m3")
    return (out_0,) + planes(out_0)

@@ -1,0 +1,328 @@
+from contextlib import ExitStack
+
+import concourse.mybir as mybir
+
+K, T, S, N, H, U = 1024, 2048, 512, 512, 512, 1024
+FLOPS = 2 * K * N * S * 2 + 2 * H * N * U
+
+F32 = mybir.dt.float32
+BF16 = mybir.dt.bfloat16
+I32 = mybir.dt.int32
+U32 = mybir.dt.uint32
+U16 = mybir.dt.uint16
+U8 = mybir.dt.uint8
+FP8X4 = mybir.dt.float8_e4m3fn_x4
+FP4X4 = mybir.dt.float4_e2m1fn_x4
+ALU = mybir.AluOpType
+COPY = mybir.ActivationFunctionType.Copy
+
+P = 128
+PACK = 4
+PASSES = K // (P * PACK)
+BLOCK = 128
+CHUNKS = (384, 384, 128, 128)
+ROUND_ON_SCALAR = (0, 1)
+Z_ON_VECTOR = (0, 1)
+
+
+def load_scale_rows(queue, tile, scales):
+    for q in range(4):
+        queue.dma_start(
+            out=tile[32 * q : 32 * q + 4, :, :].bitcast(I32),
+            in_=scales[:, 4 * q : 4 * q + 4, :].rearrange("g r n -> r g n").bitcast(I32),
+        )
+
+
+def deal_words(copy, dtype, pool, name, words):
+    gm = words.shape[1] // (2 * PACK)
+    dealt = pool.tile([P, PACK, 2 * gm], U8, name=name, align_bytes=64)
+    if dtype == U16:
+        copy(out=dealt[:].bitcast(U16), in_=words.bitcast(U16).rearrange("p (m t) -> p t m", t=PACK))
+    else:
+        copy(
+            out=dealt[:].rearrange("p t (m b) -> p t m b", b=2),
+            in_=words.rearrange("p (m t b) -> p t m b", t=PACK, b=2),
+        )
+    return dealt
+
+
+def deal_scales(copy, pool, name, scales):
+    gm = scales.shape[1] * scales.shape[2] // PACK
+    dealt = pool.tile([P, PACK, gm], U8, name=name, align_bytes=64)
+    copy(out=dealt[:], in_=scales.rearrange("p g (m t) -> p t (g m)", t=PACK))
+    return dealt
+
+
+def tile_picked_ydelayq_mul_po_kernel(
+    tc, x_words, x_scales, w1_words, w1_scales, w2_words, w2_scales, unit, w3_words, w3_scales, offs, bk, rw_, out_0, out_1, out_2
+):
+    nc = tc.nc
+    with ExitStack() as ctx:
+        keep = ctx.enter_context(tc.tile_pool(name="keep", bufs=1))
+        psum = ctx.enter_context(tc.psum_pool(name="psum", bufs=1))
+
+        offs_sb = keep.tile([P, S // 16], U16, name="offs_sb")
+        bk_sb = keep.tile([P, U // 16], U16, name="bk_sb")
+        rw_sb = keep.tile([P, U // 16], U16, name="rw_sb")
+        xw = [keep.tile([P, T], U32, name=f"xw{g}", align_bytes=64) for g in range(PASSES)]
+        xs = keep.tile([P, T], U8, name="xs", align_bytes=64)
+        xq_planes = keep.tile([P, PASSES, S], U8, name="xq_planes", align_bytes=64)
+        w1w = keep.tile([P, PASSES * 2 * N], U8, name="w1w", align_bytes=64)
+        w2w = keep.tile([P, PASSES * 2 * N], U8, name="w2w", align_bytes=64)
+        w1s = keep.tile([P, PASSES, N], U8, name="w1s", align_bytes=64)
+        w2s = keep.tile([P, PASSES, N], U8, name="w2s", align_bytes=64)
+        unit_sb = keep.tile([P, PACK], F32, name="unit_sb")
+
+        nc.gpsimd.memset(w1s[:].bitcast(I32), 0)
+        nc.gpsimd.memset(w2s[:].bitcast(I32), 0)
+        nc.vector.memset(xs[32:64, :].bitcast(I32), 0)
+        nc.vector.memset(xs[64:128, :].bitcast(I32), 0)
+        nc.vector.memset(xq_planes[:].bitcast(I32), 0)
+
+        def load_words(tile, words):
+            nc.sync.dma_start(
+                out=tile.rearrange("p (g n) -> p g n", g=words.shape[0]).bitcast(I32),
+                in_=words.rearrange("g p n -> p g n").bitcast(I32),
+            )
+
+        def load_x(g):
+            nc.sync.dma_start(out=xw[g][:].bitcast(I32), in_=x_words[g].rearrange("p n t -> p (n t)").bitcast(I32))
+
+        nc.sync.dma_start(offs_sb[:], offs)
+        nc.sync.dma_start(out=xs[0:32, :].bitcast(I32), in_=x_scales.rearrange("g r n -> r g n").bitcast(I32))
+        load_x(0)
+        load_words(w1w[:], w1_words)
+        load_x(1)
+        load_words(w2w[:], w2_words)
+        nc.sync.dma_start(bk_sb[:], bk)
+        nc.sync.dma_start(rw_sb[:], rw_)
+        load_scale_rows(nc.gpsimd, w1s[:], w1_scales)
+        load_scale_rows(nc.gpsimd, w2s[:], w2_scales)
+        nc.gpsimd.dma_start(out=unit_sb[:], in_=unit.rearrange("(p t) o -> p (t o)", t=PACK))
+
+        xq_words = [keep.tile([P, S], U32, name=f"xq_words{g}", align_bytes=64) for g in range(PASSES)]
+        xq_rows = keep.tile([P, S], U8, name="xq_rows", align_bytes=64)
+        nc.vector.tensor_copy(out=xq_rows[:], in_=xs[:].indirect(offs_sb[:]))
+        for q in range(4):
+            nc.scalar.dma_start(out=xq_planes[32 * q : 32 * q + 4, :, :].bitcast(I32), in_=xq_rows[8 * q : 8 * q + 8, :].bitcast(I32))
+        nc.vector.tensor_copy(out=xq_words[0][:], in_=xw[0][:].indirect(offs_sb[:]))
+        w1_dealt = deal_words(nc.scalar.copy, U16, keep, "w1_dealt", w1w[:])
+        w1_planes = deal_scales(nc.vector.tensor_copy, keep, "w1_planes", w1s[:])
+        nc.vector.tensor_copy(out=xq_words[1][:], in_=xw[1][:].indirect(offs_sb[:]))
+        w2_dealt = deal_words(nc.vector.tensor_copy, U16, keep, "w2_dealt", w2w[:])
+        w3w = w1w[:, 0 : 2 * N]
+        w3s = w1s[:, 0:1, :]
+        load_words(w3w, w3_words)
+        load_scale_rows(nc.sync, w3s, w3_scales)
+        w2_planes = deal_scales(nc.vector.tensor_copy, keep, "w2_planes", w2s[:])
+
+        def first_product(bank, words, scales):
+            acc = psum.tile([P, S], F32, name=f"acc{bank}", tag=f"bank{bank}")
+            for g in range(PASSES):
+                nc.tensor.matmul_mx(
+                    out=acc[:],
+                    lhsT=words[:, 256 * g : 256 * (g + 1)].bitcast(FP4X4),
+                    lhsT_scale=scales[:, 128 * g : 128 * (g + 1)],
+                    rhs=xq_words[g][:].bitcast(FP8X4),
+                    rhs_scale=xq_planes[:, g, :],
+                    start=(g == 0),
+                    stop=(g == PASSES - 1),
+                )
+            return acc
+
+        y_ps = {}
+        z_ps = {}
+        for t in (0, 1):
+            y_ps[t] = first_product(t, w1_dealt[:, t, :], w1_planes[:, t, :])
+        for t in (0, 1):
+            z_ps[t] = first_product(PACK + t, w2_dealt[:, t, :], w2_planes[:, t, :])
+        for t in (2, 3):
+            y_ps[t] = first_product(t, w1_dealt[:, t, :], w1_planes[:, t, :])
+        for t in (2, 3):
+            z_ps[t] = first_product(PACK + t, w2_dealt[:, t, :], w2_planes[:, t, :])
+        y = [keep.tile([P, S], F32, name=f"y{t}", align_bytes=64) for t in range(PACK)]
+        z = [keep.tile([P, S], F32, name=f"z{t}", align_bytes=64) for t in range(PACK)]
+
+        out_scales = keep.tile([P, U], U8, name="out_scales", align_bytes=64)
+        out_rows = out_0.rearrange("(p t) r -> p t r", t=PACK)
+        out_words = out_1[0].rearrange("p r t -> p (r t)").bitcast(I32)
+        starts = [sum(CHUNKS[:c]) for c in range(len(CHUNKS))]
+
+        def per_chunk(name, dtype, shape):
+            return [keep.tile(shape(n), dtype, name=f"{name}{c}", align_bytes=64) for c, n in enumerate(CHUNKS)]
+
+        yk = per_chunk("yk", F32, lambda n: [P, PACK, n])
+        yr = per_chunk("yr", F32, lambda n: [P, PACK, n])
+        busy = per_chunk("busy", F32, lambda n: [P, PACK, n])
+        prod = per_chunk("prod", F32, lambda n: [P, PACK, n])
+        hid = per_chunk("hid", F32, lambda n: [P, PACK, n])
+        hid_bf = per_chunk("hid_bf", BF16, lambda n: [P, n, PACK])
+        hid_codes = per_chunk("hid_codes", U32, lambda n: [P, n])
+        hid_scales = per_chunk("hid_scales", U8, lambda n: [P, n])
+        out_sb = per_chunk("out_sb", F32, lambda n: [P, PACK, n])
+        out_bf = per_chunk("out_bf", BF16, lambda n: [P, n, PACK])
+        out_codes = per_chunk("out_codes", U32, lambda n: [P, n])
+        out_ps = {}
+
+        def entries(lst, c):
+            return lst[:, starts[c] // 16 : (starts[c] + CHUNKS[c]) // 16]
+
+        def y_out(t):
+            nc.scalar.activation(out=y[t][:], in_=y_ps[t][:], func=COPY)
+
+        def z_out_scalar(t):
+            nc.scalar.activation(out=z[t][:], in_=z_ps[t][:], func=COPY, scale=unit_sb[:, t : t + 1])
+
+        def z_out_vector(t):
+            nc.vector.tensor_scalar(out=z[t][:], in0=z_ps[t][:], scalar1=unit_sb[:, t : t + 1], scalar2=None, op0=ALU.mult)
+
+        def fetch_k(c, t):
+            nc.scalar.activation(out=yk[c][:, t, :], in_=y[t][:].indirect(entries(bk_sb, c)), func=COPY)
+
+        def fetch_r(c, t):
+            nc.scalar.activation(out=yr[c][:, t, :], in_=y[t][:].indirect(entries(rw_sb, c)), func=COPY)
+
+        def fetch_r_vector(c, t):
+            nc.vector.tensor_copy(out=yr[c][:, t, :], in_=y[t][:].indirect(entries(rw_sb, c)))
+
+        def fetch(c, ts):
+            for t in ts:
+                fetch_k(c, t)
+                fetch_r(c, t)
+
+        def later(c, t0, t1):
+            nc.vector.tensor_tensor(out=busy[c][:, t0:t1, :], in0=yk[c][:, t0:t1, :], in1=yr[c][:, t0:t1, :], op=ALU.max)
+
+        def times(c, t):
+            nc.vector.tensor_tensor(out=prod[c][:, t, :], in0=z[t][:].indirect(entries(bk_sb, c)), in1=busy[c][:, t, :], op=ALU.mult)
+
+        def plus(c, t):
+            nc.vector.tensor_tensor(out=hid[c][:, t, :], in0=z[t][:].indirect(entries(rw_sb, c)), in1=prod[c][:, t, :], op=ALU.add)
+
+        def interleave(dst, src):
+            nc.vector.tensor_copy(
+                out=dst.rearrange("p (c i) t -> p c t i", i=4),
+                in_=src.rearrange("p t (c i) -> p c t i", i=4),
+            )
+
+        def round_hid(c):
+            interleave(hid_bf[c][:], hid[c][:])
+
+        def last_product(c):
+            nc.vector.quantize_mx(out=hid_codes[c][:].bitcast(FP8X4), scales=hid_scales[c][:], in_=hid_bf[c][:].rearrange("p r t -> p (r t)"))
+            for b in range(CHUNKS[c] // BLOCK):
+                bank = starts[c] // BLOCK + b
+                acc = psum.tile([P, PACK, BLOCK], F32, name=f"out_ps{bank}", tag=f"bank{bank}")
+                cols = slice(b * BLOCK, (b + 1) * BLOCK)
+                for t in range(PACK):
+                    nc.tensor.matmul_mx(
+                        out=acc[:, t, :],
+                        lhsT=w3_dealt[:, t, :].bitcast(FP4X4),
+                        lhsT_scale=w3_planes[:, t, :],
+                        rhs=hid_codes[c][:, cols].bitcast(FP8X4),
+                        rhs_scale=hid_scales[c][:, cols],
+                        start=True,
+                        stop=True,
+                    )
+                out_ps[(c, b)] = acc
+
+        def store_values(c):
+            n = CHUNKS[c]
+            for b in range(n // BLOCK):
+                nc.scalar.activation(out=out_sb[c][:, :, b * BLOCK : (b + 1) * BLOCK], in_=out_ps[(c, b)][:], func=COPY)
+            nc.sync.dma_start(out=out_rows[:, :, starts[c] : starts[c] + n], in_=out_sb[c][:])
+
+        def round_out_scalar(c):
+            for b in range(CHUNKS[c] // BLOCK):
+                nc.scalar.activation(
+                    out=out_bf[c][:, b * BLOCK : (b + 1) * BLOCK, :], in_=out_ps[(c, b)][:].rearrange("p t r -> p r t"), func=COPY
+                )
+
+        def round_out_vector(c):
+            interleave(out_bf[c][:], out_sb[c][:])
+
+        def round_out_vector_psum(c):
+            nc.vector.tensor_copy(out=out_bf[c][:], in_=out_ps[(c, 0)][:].rearrange("p t r -> p r t"))
+
+        def store_planes(c):
+            cols = slice(starts[c], starts[c] + CHUNKS[c])
+            nc.vector.quantize_mx(out=out_codes[c][:].bitcast(FP8X4), scales=out_scales[:, cols], in_=out_bf[c][:].rearrange("p r t -> p (r t)"))
+            nc.sync.dma_start(out=out_words[:, cols], in_=out_codes[c][:].bitcast(I32))
+
+        y_out(0)
+        y_out(1)
+        fetch_k(0, 0)
+        fetch_r_vector(0, 0)
+        fetch(0, [1])
+        z_out_vector(0)
+        later(0, 0, 1)
+        z_out_vector(1)
+        y_out(2)
+        y_out(3)
+        z_out_scalar(2)
+        fetch(0, [2])
+        z_out_scalar(3)
+        fetch(0, [3])
+        times(0, 0)
+        later(0, 1, 2)
+        plus(0, 0)
+        times(0, 1)
+        w3_dealt = deal_words(nc.vector.tensor_copy, U16, keep, "w3_dealt", w3w)
+        plus(0, 1)
+        later(0, 2, 4)
+        w3_planes = deal_scales(nc.vector.tensor_copy, keep, "w3_planes", w3s)
+        fetch(1, [0, 1])
+        times(0, 2)
+        times(0, 3)
+        later(1, 0, 2)
+        plus(0, 2)
+        plus(0, 3)
+        fetch(1, [2, 3])
+        times(1, 0)
+        round_hid(0)
+        times(1, 1)
+        last_product(0)
+        later(1, 2, 4)
+        plus(1, 0)
+        plus(1, 1)
+        fetch(2, [0, 1, 2, 3])
+        store_values(0)
+        round_out_scalar(0)
+        fetch(3, [0, 1, 2, 3])
+        times(1, 2)
+        times(1, 3)
+        later(2, 0, 4)
+        plus(1, 2)
+        plus(1, 3)
+        times(2, 0)
+        round_hid(1)
+        times(2, 1)
+        last_product(1)
+        times(2, 2)
+        store_planes(0)
+        times(2, 3)
+        later(3, 0, 4)
+        store_values(1)
+        round_out_scalar(1)
+        for t in range(PACK):
+            plus(2, t)
+        times(3, 0)
+        round_hid(2)
+        times(3, 1)
+        last_product(2)
+        times(3, 2)
+        times(3, 3)
+        store_values(2)
+        round_out_scalar(2)
+        for t in range(PACK):
+            plus(3, t)
+        store_planes(1)
+        round_hid(3)
+        store_planes(2)
+        last_product(3)
+        round_out_vector_psum(3)
+        store_values(3)
+        store_planes(3)
+        for q in range(4):
+            queue = nc.sync if q % 2 == 0 else nc.scalar
+            queue.dma_start(out=out_2[0, 4 * q : 4 * q + 4, :].bitcast(I32), in_=out_scales[32 * q : 32 * q + 4, :].bitcast(I32))

@@ -33,24 +33,12 @@ def load_scale_rows(queue, tile, scales):
         )
 
 
-def deal_words(copy, dtype, pool, name, words):
-    gm = words.shape[1] // (2 * PACK)
-    dealt = pool.tile([P, PACK, 2 * gm], U8, name=name, align_bytes=64)
-    if dtype == U16:
-        copy(out=dealt[:].bitcast(U16), in_=words.bitcast(U16).rearrange("p (m t) -> p t m", t=PACK))
-    else:
-        copy(
-            out=dealt[:].rearrange("p t (m b) -> p t m b", b=2),
-            in_=words.rearrange("p (m t b) -> p t m b", t=PACK, b=2),
-        )
-    return dealt
+def deal_words(copy, dealt, words):
+    copy(out=dealt.bitcast(U16), in_=words.bitcast(U16).rearrange("p (m t) -> p t m", t=PACK))
 
 
-def deal_scales(copy, pool, name, scales):
-    gm = scales.shape[1] * scales.shape[2] // PACK
-    dealt = pool.tile([P, PACK, gm], U8, name=name, align_bytes=64)
-    copy(out=dealt[:], in_=scales.rearrange("p g (m t) -> p t (g m)", t=PACK))
-    return dealt
+def deal_scales(copy, dealt, scales):
+    copy(out=dealt, in_=scales.rearrange("p g (m t) -> p t (g m)", t=PACK))
 
 
 def tile_picked_ydelayq_mul_po_kernel(
@@ -64,10 +52,9 @@ def tile_picked_ydelayq_mul_po_kernel(
         offs_sb = keep.tile([P, S // 16], U16, name="offs_sb")
         bk_sb = keep.tile([P, U // 16], U16, name="bk_sb")
         rw_sb = keep.tile([P, U // 16], U16, name="rw_sb")
-        xw = [keep.tile([P, T], U32, name=f"xw{g}", align_bytes=64) for g in range(PASSES)]
+        xw = [keep.tile([P, T], U32, name=f"xw{g}", tag=f"xw{g}", align_bytes=64) for g in range(PASSES)]
         xs = keep.tile([P, T], U8, name="xs", align_bytes=64)
-        xq_planes = keep.tile([P, PASSES, S], U8, name="xq_planes", align_bytes=64)
-        w1w = keep.tile([P, PASSES * 2 * N], U8, name="w1w", align_bytes=64)
+        w1w = keep.tile([P, PASSES * 2 * N], U8, name="w1w", tag="w1w", align_bytes=64)
         w2w = keep.tile([P, PASSES * 2 * N], U8, name="w2w", align_bytes=64)
         w1s = keep.tile([P, PASSES, N], U8, name="w1s", align_bytes=64)
         w2s = keep.tile([P, PASSES, N], U8, name="w2s", align_bytes=64)
@@ -77,7 +64,6 @@ def tile_picked_ydelayq_mul_po_kernel(
         nc.gpsimd.memset(w2s[:].bitcast(I32), 0)
         nc.vector.memset(xs[32:64, :].bitcast(I32), 0)
         nc.vector.memset(xs[64:128, :].bitcast(I32), 0)
-        nc.vector.memset(xq_planes[:].bitcast(I32), 0)
 
         def load_words(tile, words):
             nc.sync.dma_start(
@@ -90,31 +76,40 @@ def tile_picked_ydelayq_mul_po_kernel(
 
         nc.sync.dma_start(offs_sb[:], offs)
         nc.sync.dma_start(out=xs[0:32, :].bitcast(I32), in_=x_scales.rearrange("g r n -> r g n").bitcast(I32))
-        load_x(0)
         load_words(w1w[:], w1_words)
-        load_x(1)
+        load_x(0)
         load_words(w2w[:], w2_words)
+        load_x(1)
         nc.sync.dma_start(bk_sb[:], bk)
         nc.sync.dma_start(rw_sb[:], rw_)
-        load_scale_rows(nc.gpsimd, w1s[:], w1_scales)
+        load_scale_rows(nc.scalar, w1s[:], w1_scales)
         load_scale_rows(nc.gpsimd, w2s[:], w2_scales)
         nc.gpsimd.dma_start(out=unit_sb[:], in_=unit.rearrange("(p t) o -> p (t o)", t=PACK))
 
         xq_words = [keep.tile([P, S], U32, name=f"xq_words{g}", align_bytes=64) for g in range(PASSES)]
         xq_rows = keep.tile([P, S], U8, name="xq_rows", align_bytes=64)
         nc.vector.tensor_copy(out=xq_rows[:], in_=xs[:].indirect(offs_sb[:]))
+        w1_dealt = keep.tile([P, PACK, 512], U8, name="w1_dealt", align_bytes=64)
+        deal_words(nc.scalar.copy, w1_dealt[:], w1w[:])
+        xq_planes = keep.tile([P, PASSES, S], U8, name="xq_planes", tag="w1w", align_bytes=64)
+        nc.vector.memset(xq_planes[:].bitcast(I32), 0)
         for q in range(4):
             nc.scalar.dma_start(out=xq_planes[32 * q : 32 * q + 4, :, :].bitcast(I32), in_=xq_rows[8 * q : 8 * q + 8, :].bitcast(I32))
         nc.vector.tensor_copy(out=xq_words[0][:], in_=xw[0][:].indirect(offs_sb[:]))
-        w1_dealt = deal_words(nc.scalar.copy, U16, keep, "w1_dealt", w1w[:])
-        w1_planes = deal_scales(nc.vector.tensor_copy, keep, "w1_planes", w1s[:])
+        w1_planes = keep.tile([P, PACK, 256], U8, name="w1_planes", align_bytes=64)
+        deal_scales(nc.vector.tensor_copy, w1_planes[:], w1s[:])
+        w2_dealt = keep.tile([P, PACK, 512], U8, name="w2_dealt", align_bytes=64)
+        deal_words(nc.scalar.copy, w2_dealt[:], w2w[:])
         nc.vector.tensor_copy(out=xq_words[1][:], in_=xw[1][:].indirect(offs_sb[:]))
-        w2_dealt = deal_words(nc.vector.tensor_copy, U16, keep, "w2_dealt", w2w[:])
-        w3w = w1w[:, 0 : 2 * N]
+        late = keep.tile([P, 2560], U8, name="late", tag="xw1", align_bytes=64)
+        w2_planes = late[:, 0:1024].rearrange("p (t n) -> p t n", t=PACK)
+        w3_dealt = late[:, 1024:2048].rearrange("p (t n) -> p t n", t=PACK)
+        w3_planes = late[:, 2048:2560].rearrange("p (t n) -> p t n", t=PACK)
+        w3w = w2w[:, 0 : 2 * N]
         w3s = w1s[:, 0:1, :]
         load_words(w3w, w3_words)
         load_scale_rows(nc.sync, w3s, w3_scales)
-        w2_planes = deal_scales(nc.vector.tensor_copy, keep, "w2_planes", w2s[:])
+        deal_scales(nc.vector.tensor_copy, w2_planes, w2s[:])
 
         def first_product(bank, words, scales):
             acc = psum.tile([P, S], F32, name=f"acc{bank}", tag=f"bank{bank}")
@@ -162,6 +157,8 @@ def tile_picked_ydelayq_mul_po_kernel(
         out_sb = per_chunk("out_sb", F32, lambda n: [P, PACK, n])
         out_bf = per_chunk("out_bf", BF16, lambda n: [P, n, PACK])
         out_codes = per_chunk("out_codes", U32, lambda n: [P, n])
+        zk = keep.tile([P, PACK, CHUNKS[-1]], F32, name="zk", align_bytes=64)
+        zr = keep.tile([P, PACK, CHUNKS[-1]], F32, name="zr", align_bytes=64)
         out_ps = {}
 
         def entries(lst, c):
@@ -184,6 +181,18 @@ def tile_picked_ydelayq_mul_po_kernel(
 
         def fetch_r_vector(c, t):
             nc.vector.tensor_copy(out=yr[c][:, t, :], in_=y[t][:].indirect(entries(rw_sb, c)))
+
+        def fetch_z(c):
+            for t in range(PACK):
+                nc.scalar.activation(out=zk[:, t, :], in_=z[t][:].indirect(entries(bk_sb, c)), func=COPY)
+            for t in range(PACK):
+                nc.scalar.activation(out=zr[:, t, :], in_=z[t][:].indirect(entries(rw_sb, c)), func=COPY)
+
+        def times_fetched(c):
+            nc.vector.tensor_tensor(out=prod[c][:], in0=zk[:], in1=busy[c][:], op=ALU.mult)
+
+        def plus_fetched(c):
+            nc.vector.tensor_tensor(out=hid[c][:], in0=zr[:], in1=prod[c][:], op=ALU.add)
 
         def fetch(c, ts):
             for t in ts:
@@ -259,7 +268,6 @@ def tile_picked_ydelayq_mul_po_kernel(
         z_out_vector(1)
         y_out(2)
         y_out(3)
-        z_out_scalar(2)
         fetch(0, [2])
         z_out_scalar(3)
         fetch(0, [3])
@@ -267,21 +275,23 @@ def tile_picked_ydelayq_mul_po_kernel(
         later(0, 1, 2)
         plus(0, 0)
         times(0, 1)
-        w3_dealt = deal_words(nc.vector.tensor_copy, U16, keep, "w3_dealt", w3w)
+        z_out_vector(2)
         plus(0, 1)
-        later(0, 2, 4)
-        w3_planes = deal_scales(nc.vector.tensor_copy, keep, "w3_planes", w3s)
-        fetch(1, [0, 1])
+        later(0, 2, 3)
+        deal_words(nc.vector.tensor_copy, w3_dealt, w3w)
         times(0, 2)
-        times(0, 3)
-        later(1, 0, 2)
+        later(0, 3, 4)
         plus(0, 2)
+        times(0, 3)
+        deal_scales(nc.vector.tensor_copy, w3_planes, w3s)
         plus(0, 3)
-        fetch(1, [2, 3])
-        times(1, 0)
+        fetch(1, [0, 1])
+        later(1, 0, 2)
         round_hid(0)
-        times(1, 1)
+        times(1, 0)
         last_product(0)
+        times(1, 1)
+        fetch(1, [2, 3])
         later(1, 2, 4)
         plus(1, 0)
         plus(1, 1)
@@ -289,6 +299,7 @@ def tile_picked_ydelayq_mul_po_kernel(
         store_values(0)
         round_out_scalar(0)
         fetch(3, [0, 1, 2, 3])
+        fetch_z(3)
         times(1, 2)
         times(1, 3)
         later(2, 0, 4)
@@ -301,26 +312,24 @@ def tile_picked_ydelayq_mul_po_kernel(
         times(2, 2)
         store_planes(0)
         times(2, 3)
-        later(3, 0, 4)
         store_values(1)
         round_out_scalar(1)
-        for t in range(PACK):
-            plus(2, t)
-        times(3, 0)
+        plus(2, 0)
+        plus(2, 1)
+        later(3, 0, 4)
+        plus(2, 2)
+        plus(2, 3)
+        times_fetched(3)
         round_hid(2)
-        times(3, 1)
+        plus_fetched(3)
         last_product(2)
-        times(3, 2)
-        times(3, 3)
-        store_values(2)
-        round_out_scalar(2)
-        for t in range(PACK):
-            plus(3, t)
-        store_planes(1)
         round_hid(3)
-        store_planes(2)
+        store_values(2)
+        store_planes(1)
         last_product(3)
+        round_out_vector(2)
         round_out_vector_psum(3)
+        store_planes(2)
         store_values(3)
         store_planes(3)
         for q in range(4):

@@ -37,8 +37,8 @@ def deal_words(copy, dealt, words):
     copy(out=dealt.bitcast(U16), in_=words.bitcast(U16).rearrange("p (m t) -> p t m", t=PACK))
 
 
-def deal_scales(copy, dealt, scales):
-    copy(out=dealt, in_=scales.rearrange("p g (m t) -> p t (g m)", t=PACK))
+def deal_scales(copy, dealt, scales, t0):
+    copy(out=dealt, in_=scales.rearrange("p g (m t) -> p t (g m)", t=PACK)[:, t0 : t0 + dealt.shape[1], :])
 
 
 def tile_picked_ydelayq_mul_po_kernel(
@@ -54,7 +54,8 @@ def tile_picked_ydelayq_mul_po_kernel(
         rw_sb = keep.tile([P, U // 16], U16, name="rw_sb")
         xw = [keep.tile([P, T], U32, name=f"xw{g}", tag=f"xw{g}", align_bytes=64) for g in range(PASSES)]
         xs = keep.tile([P, T], U8, name="xs", align_bytes=64)
-        w1w = keep.tile([P, PASSES * 2 * N], U8, name="w1w", tag="w1w", align_bytes=64)
+        xq_planes = keep.tile([P, PASSES, S], U8, name="xq_planes", align_bytes=64)
+        w1w = keep.tile([P, PASSES * 2 * N], U8, name="w1w", align_bytes=64)
         w2w = keep.tile([P, PASSES * 2 * N], U8, name="w2w", align_bytes=64)
         w1s = keep.tile([P, PASSES, N], U8, name="w1s", align_bytes=64)
         w2s = keep.tile([P, PASSES, N], U8, name="w2s", align_bytes=64)
@@ -64,6 +65,7 @@ def tile_picked_ydelayq_mul_po_kernel(
         nc.gpsimd.memset(w2s[:].bitcast(I32), 0)
         nc.vector.memset(xs[32:64, :].bitcast(I32), 0)
         nc.vector.memset(xs[64:128, :].bitcast(I32), 0)
+        nc.vector.memset(xq_planes[:].bitcast(I32), 0)
 
         def load_words(tile, words):
             nc.sync.dma_start(
@@ -77,39 +79,40 @@ def tile_picked_ydelayq_mul_po_kernel(
         nc.sync.dma_start(offs_sb[:], offs)
         nc.sync.dma_start(out=xs[0:32, :].bitcast(I32), in_=x_scales.rearrange("g r n -> r g n").bitcast(I32))
         load_words(w1w[:], w1_words)
+        load_scale_rows(nc.sync, w1s[:], w1_scales)
         load_x(0)
-        load_words(w2w[:], w2_words)
         load_x(1)
+        load_words(w2w[:], w2_words)
         nc.sync.dma_start(bk_sb[:], bk)
         nc.sync.dma_start(rw_sb[:], rw_)
-        load_scale_rows(nc.scalar, w1s[:], w1_scales)
         load_scale_rows(nc.gpsimd, w2s[:], w2_scales)
         nc.gpsimd.dma_start(out=unit_sb[:], in_=unit.rearrange("(p t) o -> p (t o)", t=PACK))
 
         xq_words = [keep.tile([P, S], U32, name=f"xq_words{g}", align_bytes=64) for g in range(PASSES)]
         xq_rows = keep.tile([P, S], U8, name="xq_rows", align_bytes=64)
         nc.vector.tensor_copy(out=xq_rows[:], in_=xs[:].indirect(offs_sb[:]))
-        w1_dealt = keep.tile([P, PACK, 512], U8, name="w1_dealt", align_bytes=64)
-        deal_words(nc.scalar.copy, w1_dealt[:], w1w[:])
-        xq_planes = keep.tile([P, PASSES, S], U8, name="xq_planes", tag="w1w", align_bytes=64)
-        nc.vector.memset(xq_planes[:].bitcast(I32), 0)
         for q in range(4):
             nc.scalar.dma_start(out=xq_planes[32 * q : 32 * q + 4, :, :].bitcast(I32), in_=xq_rows[8 * q : 8 * q + 8, :].bitcast(I32))
         nc.vector.tensor_copy(out=xq_words[0][:], in_=xw[0][:].indirect(offs_sb[:]))
-        w1_planes = keep.tile([P, PACK, 256], U8, name="w1_planes", align_bytes=64)
-        deal_scales(nc.vector.tensor_copy, w1_planes[:], w1s[:])
+        w1_dealt = keep.tile([P, PACK, 512], U8, name="w1_dealt", align_bytes=64)
+        w1_first = keep.tile([P, 2, 256], U8, name="w1_first", align_bytes=64)
+        deal_words(nc.scalar.copy, w1_dealt[:], w1w[:])
+        deal_scales(nc.vector.tensor_copy, w1_first[:], w1s[:], 0)
         w2_dealt = keep.tile([P, PACK, 512], U8, name="w2_dealt", align_bytes=64)
         deal_words(nc.scalar.copy, w2_dealt[:], w2w[:])
         nc.vector.tensor_copy(out=xq_words[1][:], in_=xw[1][:].indirect(offs_sb[:]))
-        late = keep.tile([P, 2560], U8, name="late", tag="xw1", align_bytes=64)
+        late = keep.tile([P, 3072], U8, name="late", tag="xw1", align_bytes=64)
         w2_planes = late[:, 0:1024].rearrange("p (t n) -> p t n", t=PACK)
         w3_dealt = late[:, 1024:2048].rearrange("p (t n) -> p t n", t=PACK)
         w3_planes = late[:, 2048:2560].rearrange("p (t n) -> p t n", t=PACK)
-        w3w = w2w[:, 0 : 2 * N]
+        w1_second = late[:, 2560:3072].rearrange("p (t n) -> p t n", t=2)
+        deal_scales(nc.vector.tensor_copy, w2_planes, w2s[:], 0)
+        deal_scales(nc.vector.tensor_copy, w1_second, w1s[:], 2)
+        w1_planes = [w1_first[:, 0, :], w1_first[:, 1, :], w1_second[:, 0, :], w1_second[:, 1, :]]
+        w3w = w1w[:, 0 : 2 * N]
         w3s = w1s[:, 0:1, :]
         load_words(w3w, w3_words)
         load_scale_rows(nc.sync, w3s, w3_scales)
-        deal_scales(nc.vector.tensor_copy, w2_planes, w2s[:])
 
         def first_product(bank, words, scales):
             acc = psum.tile([P, S], F32, name=f"acc{bank}", tag=f"bank{bank}")
@@ -128,11 +131,11 @@ def tile_picked_ydelayq_mul_po_kernel(
         y_ps = {}
         z_ps = {}
         for t in (0, 1):
-            y_ps[t] = first_product(t, w1_dealt[:, t, :], w1_planes[:, t, :])
+            y_ps[t] = first_product(t, w1_dealt[:, t, :], w1_planes[t])
         for t in (0, 1):
             z_ps[t] = first_product(PACK + t, w2_dealt[:, t, :], w2_planes[:, t, :])
         for t in (2, 3):
-            y_ps[t] = first_product(t, w1_dealt[:, t, :], w1_planes[:, t, :])
+            y_ps[t] = first_product(t, w1_dealt[:, t, :], w1_planes[t])
         for t in (2, 3):
             z_ps[t] = first_product(PACK + t, w2_dealt[:, t, :], w2_planes[:, t, :])
         y = [keep.tile([P, S], F32, name=f"y{t}", align_bytes=64) for t in range(PACK)]
@@ -239,7 +242,8 @@ def tile_picked_ydelayq_mul_po_kernel(
             n = CHUNKS[c]
             for b in range(n // BLOCK):
                 nc.scalar.activation(out=out_sb[c][:, :, b * BLOCK : (b + 1) * BLOCK], in_=out_ps[(c, b)][:], func=COPY)
-            nc.sync.dma_start(out=out_rows[:, :, starts[c] : starts[c] + n], in_=out_sb[c][:])
+            queue = nc.scalar if c == len(CHUNKS) - 1 else nc.sync
+            queue.dma_start(out=out_rows[:, :, starts[c] : starts[c] + n], in_=out_sb[c][:])
 
         def round_out_scalar(c):
             for b in range(CHUNKS[c] // BLOCK):
@@ -283,7 +287,7 @@ def tile_picked_ydelayq_mul_po_kernel(
         later(0, 3, 4)
         plus(0, 2)
         times(0, 3)
-        deal_scales(nc.vector.tensor_copy, w3_planes, w3s)
+        deal_scales(nc.vector.tensor_copy, w3_planes, w3s, 0)
         plus(0, 3)
         fetch(1, [0, 1])
         later(1, 0, 2)

@@ -33,8 +33,8 @@ def load_scale_rows(queue, tile, scales):
         )
 
 
-def deal_words(copy, dealt, words):
-    copy(out=dealt.bitcast(U16), in_=words.bitcast(U16).rearrange("p (m t) -> p t m", t=PACK))
+def deal_words(copy, dealt, words, t0):
+    copy(out=dealt.bitcast(U16), in_=words.bitcast(U16).rearrange("p (m t) -> p t m", t=PACK)[:, t0 : t0 + dealt.shape[1], :])
 
 
 def deal_scales(copy, dealt, scales, t0):
@@ -54,21 +54,19 @@ def tile_picked_ydelayq_mul_po_kernel(
         rw_sb = keep.tile([P, U // 16], U16, name="rw_sb")
         xw = [keep.tile([P, T], U32, name=f"xw{g}", tag=f"xw{g}", align_bytes=64) for g in range(PASSES)]
         xs = keep.tile([P, T], U8, name="xs", align_bytes=64)
-        xq_planes = keep.tile([P, PASSES, S], U8, name="xq_planes", align_bytes=64)
+        planes = keep.tile([P, PASSES, S + 2 * N], U8, name="planes", align_bytes=64)
         w1w = keep.tile([P, PASSES * 2 * N], U8, name="w1w", align_bytes=64)
         w2w = keep.tile([P, PASSES * 2 * N], U8, name="w2w", align_bytes=64)
-        w1s = keep.tile([P, PASSES, N], U8, name="w1s", align_bytes=64)
-        w2s = keep.tile([P, PASSES, N], U8, name="w2s", align_bytes=64)
+        ws = keep.tile([P, 2, N], U8, name="ws", align_bytes=64)
         unit_sb = keep.tile([P, PACK], F32, name="unit_sb")
 
-        nc.gpsimd.memset(w1s[:].bitcast(I32), 0)
-        nc.gpsimd.memset(w2s[:].bitcast(I32), 0)
-        nc.vector.memset(xs[32:64, :].bitcast(I32), 0)
-        nc.vector.memset(xs[64:128, :].bitcast(I32), 0)
-        nc.vector.memset(xq_planes[:].bitcast(I32), 0)
+        for lo, hi in ((32, 64), (64, 128)):
+            nc.vector.memset(xs[lo:hi, :].bitcast(I32), 0)
+            nc.vector.memset(ws[lo:hi, :, :].bitcast(I32), 0)
+        nc.vector.memset(planes[:].bitcast(I32), 0)
 
-        def load_words(tile, words):
-            nc.sync.dma_start(
+        def load_words(queue, tile, words):
+            queue.dma_start(
                 out=tile.rearrange("p (g n) -> p g n", g=words.shape[0]).bitcast(I32),
                 in_=words.rearrange("g p n -> p g n").bitcast(I32),
             )
@@ -76,53 +74,59 @@ def tile_picked_ydelayq_mul_po_kernel(
         def load_x(g):
             nc.sync.dma_start(out=xw[g][:].bitcast(I32), in_=x_words[g].rearrange("p n t -> p (n t)").bitcast(I32))
 
+        def load_rows(queue, rows, scales):
+            queue.dma_start(out=rows.bitcast(I32), in_=scales.rearrange("g r n -> r g n").bitcast(I32))
+
         nc.sync.dma_start(offs_sb[:], offs)
-        nc.sync.dma_start(out=xs[0:32, :].bitcast(I32), in_=x_scales.rearrange("g r n -> r g n").bitcast(I32))
-        load_words(w1w[:], w1_words)
-        load_scale_rows(nc.sync, w1s[:], w1_scales)
+        load_rows(nc.sync, xs[0:32, :], x_scales)
+        load_rows(nc.scalar, ws[0:32, 0, :], w1_scales)
+        load_rows(nc.scalar, ws[0:32, 1, :], w2_scales)
+        load_words(nc.sync, w1w[:], w1_words)
         load_x(0)
         load_x(1)
-        load_words(w2w[:], w2_words)
+        load_words(nc.sync, w2w[:], w2_words)
         nc.sync.dma_start(bk_sb[:], bk)
         nc.sync.dma_start(rw_sb[:], rw_)
-        load_scale_rows(nc.gpsimd, w2s[:], w2_scales)
         nc.gpsimd.dma_start(out=unit_sb[:], in_=unit.rearrange("(p t) o -> p (t o)", t=PACK))
 
         xq_words = [keep.tile([P, S], U32, name=f"xq_words{g}", align_bytes=64) for g in range(PASSES)]
         xq_rows = keep.tile([P, S], U8, name="xq_rows", align_bytes=64)
+        rows = keep.tile([P, S + 2 * N], U8, name="rows", align_bytes=64)
+        nc.vector.tensor_copy(
+            out=rows[:, S:].rearrange("p (w t m) -> p w t m", w=2, t=PACK), in_=ws[:].rearrange("p w (m t) -> p w t m", t=PACK)
+        )
         nc.vector.tensor_copy(out=xq_rows[:], in_=xs[:].indirect(offs_sb[:]))
+        nc.vector.tensor_copy(out=rows[:, 0:S], in_=xq_rows[:])
         for q in range(4):
-            nc.scalar.dma_start(out=xq_planes[32 * q : 32 * q + 4, :, :].bitcast(I32), in_=xq_rows[8 * q : 8 * q + 8, :].bitcast(I32))
+            nc.scalar.dma_start(out=planes[32 * q : 32 * q + 4, :, :].bitcast(I32), in_=rows[8 * q : 8 * q + 8, :].bitcast(I32))
         nc.vector.tensor_copy(out=xq_words[0][:], in_=xw[0][:].indirect(offs_sb[:]))
-        w1_dealt = keep.tile([P, PACK, 512], U8, name="w1_dealt", align_bytes=64)
-        w1_first = keep.tile([P, 2, 256], U8, name="w1_first", align_bytes=64)
-        deal_words(nc.scalar.copy, w1_dealt[:], w1w[:])
-        deal_scales(nc.vector.tensor_copy, w1_first[:], w1s[:], 0)
-        w2_dealt = keep.tile([P, PACK, 512], U8, name="w2_dealt", align_bytes=64)
-        deal_words(nc.scalar.copy, w2_dealt[:], w2w[:])
+        w1_first = keep.tile([P, 1, 512], U8, name="w1_first", align_bytes=64)
+        deal_words(nc.scalar.copy, w1_first[:], w1w[:], 0)
         nc.vector.tensor_copy(out=xq_words[1][:], in_=xw[1][:].indirect(offs_sb[:]))
+        w2_dealt = keep.tile([P, PACK, 512], U8, name="w2_dealt", align_bytes=64)
+        deal_words(nc.scalar.copy, w2_dealt[:], w2w[:], 0)
         late = keep.tile([P, 3072], U8, name="late", tag="xw1", align_bytes=64)
-        w2_planes = late[:, 0:1024].rearrange("p (t n) -> p t n", t=PACK)
+        w1_second = late[:, 0:1024].rearrange("p (t n) -> p t n", t=2)
         w3_dealt = late[:, 1024:2048].rearrange("p (t n) -> p t n", t=PACK)
         w3_planes = late[:, 2048:2560].rearrange("p (t n) -> p t n", t=PACK)
-        w1_second = late[:, 2560:3072].rearrange("p (t n) -> p t n", t=2)
-        deal_scales(nc.vector.tensor_copy, w2_planes, w2s[:], 0)
-        deal_scales(nc.vector.tensor_copy, w1_second, w1s[:], 2)
-        w1_planes = [w1_first[:, 0, :], w1_first[:, 1, :], w1_second[:, 0, :], w1_second[:, 1, :]]
+        w1_next = late[:, 2560:3072].rearrange("p (t n) -> p t n", t=1)
+        deal_words(nc.vector.tensor_copy, w1_next, w1w[:], 1)
+        deal_words(nc.vector.tensor_copy, w1_second, w1w[:], 2)
+        w1_dealt = [w1_first[:, 0, :], w1_next[:, 0, :], w1_second[:, 0, :], w1_second[:, 1, :]]
         w3w = w1w[:, 0 : 2 * N]
-        w3s = w1s[:, 0:1, :]
-        load_words(w3w, w3_words)
+        w3s = w1w[:, 2 * N : 3 * N].rearrange("p (g n) -> p g n", g=1)
+        load_words(nc.sync, w3w, w3_words)
         load_scale_rows(nc.sync, w3s, w3_scales)
 
-        def first_product(bank, words, scales):
+        def first_product(bank, words, scale_column):
             acc = psum.tile([P, S], F32, name=f"acc{bank}", tag=f"bank{bank}")
             for g in range(PASSES):
                 nc.tensor.matmul_mx(
                     out=acc[:],
                     lhsT=words[:, 256 * g : 256 * (g + 1)].bitcast(FP4X4),
-                    lhsT_scale=scales[:, 128 * g : 128 * (g + 1)],
+                    lhsT_scale=planes[:, g, scale_column : scale_column + 128],
                     rhs=xq_words[g][:].bitcast(FP8X4),
-                    rhs_scale=xq_planes[:, g, :],
+                    rhs_scale=planes[:, g, 0:S],
                     start=(g == 0),
                     stop=(g == PASSES - 1),
                 )
@@ -131,13 +135,13 @@ def tile_picked_ydelayq_mul_po_kernel(
         y_ps = {}
         z_ps = {}
         for t in (0, 1):
-            y_ps[t] = first_product(t, w1_dealt[:, t, :], w1_planes[t])
+            y_ps[t] = first_product(t, w1_dealt[t], S + 128 * t)
         for t in (0, 1):
-            z_ps[t] = first_product(PACK + t, w2_dealt[:, t, :], w2_planes[:, t, :])
+            z_ps[t] = first_product(PACK + t, w2_dealt[:, t, :], S + N + 128 * t)
         for t in (2, 3):
-            y_ps[t] = first_product(t, w1_dealt[:, t, :], w1_planes[t])
+            y_ps[t] = first_product(t, w1_dealt[t], S + 128 * t)
         for t in (2, 3):
-            z_ps[t] = first_product(PACK + t, w2_dealt[:, t, :], w2_planes[:, t, :])
+            z_ps[t] = first_product(PACK + t, w2_dealt[:, t, :], S + N + 128 * t)
         y = [keep.tile([P, S], F32, name=f"y{t}", align_bytes=64) for t in range(PACK)]
         z = [keep.tile([P, S], F32, name=f"z{t}", align_bytes=64) for t in range(PACK)]
 
@@ -160,8 +164,8 @@ def tile_picked_ydelayq_mul_po_kernel(
         out_sb = per_chunk("out_sb", F32, lambda n: [P, PACK, n])
         out_bf = per_chunk("out_bf", BF16, lambda n: [P, n, PACK])
         out_codes = per_chunk("out_codes", U32, lambda n: [P, n])
-        zk = keep.tile([P, PACK, CHUNKS[-1]], F32, name="zk", align_bytes=64)
-        zr = keep.tile([P, PACK, CHUNKS[-1]], F32, name="zr", align_bytes=64)
+        zk = {c: keep.tile([P, PACK, CHUNKS[c]], F32, name=f"zk{c}", align_bytes=64) for c in (3,)}
+        zr = {c: keep.tile([P, PACK, CHUNKS[c]], F32, name=f"zr{c}", align_bytes=64) for c in (2, 3)}
         out_ps = {}
 
         def entries(lst, c):
@@ -185,17 +189,19 @@ def tile_picked_ydelayq_mul_po_kernel(
         def fetch_r_vector(c, t):
             nc.vector.tensor_copy(out=yr[c][:, t, :], in_=y[t][:].indirect(entries(rw_sb, c)))
 
-        def fetch_z(c):
+        def fetch_zk(c):
             for t in range(PACK):
-                nc.scalar.activation(out=zk[:, t, :], in_=z[t][:].indirect(entries(bk_sb, c)), func=COPY)
+                nc.scalar.activation(out=zk[c][:, t, :], in_=z[t][:].indirect(entries(bk_sb, c)), func=COPY)
+
+        def fetch_zr(c):
             for t in range(PACK):
-                nc.scalar.activation(out=zr[:, t, :], in_=z[t][:].indirect(entries(rw_sb, c)), func=COPY)
+                nc.scalar.activation(out=zr[c][:, t, :], in_=z[t][:].indirect(entries(rw_sb, c)), func=COPY)
 
         def times_fetched(c):
-            nc.vector.tensor_tensor(out=prod[c][:], in0=zk[:], in1=busy[c][:], op=ALU.mult)
+            nc.vector.tensor_tensor(out=prod[c][:], in0=zk[c][:], in1=busy[c][:], op=ALU.mult)
 
         def plus_fetched(c):
-            nc.vector.tensor_tensor(out=hid[c][:], in0=zr[:], in1=prod[c][:], op=ALU.add)
+            nc.vector.tensor_tensor(out=hid[c][:], in0=zr[c][:], in1=prod[c][:], op=ALU.add)
 
         def fetch(c, ts):
             for t in ts:
@@ -245,14 +251,15 @@ def tile_picked_ydelayq_mul_po_kernel(
             queue = nc.scalar if c == len(CHUNKS) - 1 else nc.sync
             queue.dma_start(out=out_rows[:, :, starts[c] : starts[c] + n], in_=out_sb[c][:])
 
-        def round_out_scalar(c):
-            for b in range(CHUNKS[c] // BLOCK):
+        def round_out_scalar(c, blocks):
+            for b in blocks:
                 nc.scalar.activation(
                     out=out_bf[c][:, b * BLOCK : (b + 1) * BLOCK, :], in_=out_ps[(c, b)][:].rearrange("p t r -> p r t"), func=COPY
                 )
 
-        def round_out_vector(c):
-            interleave(out_bf[c][:], out_sb[c][:])
+        def round_out_vector(c, b):
+            cols = slice(b * BLOCK, (b + 1) * BLOCK)
+            interleave(out_bf[c][:, cols, :], out_sb[c][:, :, cols])
 
         def round_out_vector_psum(c):
             nc.vector.tensor_copy(out=out_bf[c][:], in_=out_ps[(c, 0)][:].rearrange("p t r -> p r t"))
@@ -282,7 +289,7 @@ def tile_picked_ydelayq_mul_po_kernel(
         z_out_vector(2)
         plus(0, 1)
         later(0, 2, 3)
-        deal_words(nc.vector.tensor_copy, w3_dealt, w3w)
+        deal_words(nc.vector.tensor_copy, w3_dealt, w3w, 0)
         times(0, 2)
         later(0, 3, 4)
         plus(0, 2)
@@ -301,9 +308,11 @@ def tile_picked_ydelayq_mul_po_kernel(
         plus(1, 1)
         fetch(2, [0, 1, 2, 3])
         store_values(0)
-        round_out_scalar(0)
+        fetch_zr(2)
+        round_out_scalar(0, (0, 1, 2))
         fetch(3, [0, 1, 2, 3])
-        fetch_z(3)
+        fetch_zk(3)
+        fetch_zr(3)
         times(1, 2)
         times(1, 3)
         later(2, 0, 4)
@@ -314,27 +323,25 @@ def tile_picked_ydelayq_mul_po_kernel(
         times(2, 1)
         last_product(1)
         times(2, 2)
-        store_planes(0)
         times(2, 3)
+        store_planes(0)
+        plus_fetched(2)
         store_values(1)
-        round_out_scalar(1)
-        plus(2, 0)
-        plus(2, 1)
         later(3, 0, 4)
-        plus(2, 2)
-        plus(2, 3)
-        times_fetched(3)
         round_hid(2)
-        plus_fetched(3)
+        times_fetched(3)
         last_product(2)
+        plus_fetched(3)
         round_hid(3)
         store_values(2)
-        store_planes(1)
+        round_out_scalar(1, (0, 1))
         last_product(3)
-        round_out_vector(2)
-        round_out_vector_psum(3)
+        round_out_vector(2, 0)
+        round_out_vector(1, 2)
         store_planes(2)
+        round_out_vector_psum(3)
         store_values(3)
+        store_planes(1)
         store_planes(3)
         for q in range(4):
             queue = nc.sync if q % 2 == 0 else nc.scalar

@@ -19,26 +19,16 @@ COPY = mybir.ActivationFunctionType.Copy
 P = 128
 PACK = 4
 PASSES = K // (P * PACK)
+QUADRANTS = 4
+LIST_ROWS = 16
+SLOT_BYTES = 2 * P
 BLOCK = 128
+LINE = 4
 CHUNKS = (384, 384, 128, 128)
-ROUND_ON_SCALAR = (0, 1)
-Z_ON_VECTOR = (0, 1)
-
-
-def load_scale_rows(queue, tile, scales):
-    for q in range(4):
-        queue.dma_start(
-            out=tile[32 * q : 32 * q + 4, :, :].bitcast(I32),
-            in_=scales[:, 4 * q : 4 * q + 4, :].rearrange("g r n -> r g n").bitcast(I32),
-        )
 
 
 def deal_words(copy, dealt, words, t0):
     copy(out=dealt.bitcast(U16), in_=words.bitcast(U16).rearrange("p (m t) -> p t m", t=PACK)[:, t0 : t0 + dealt.shape[1], :])
-
-
-def deal_scales(copy, dealt, scales, t0):
-    copy(out=dealt, in_=scales.rearrange("p g (m t) -> p t (g m)", t=PACK)[:, t0 : t0 + dealt.shape[1], :])
 
 
 def tile_picked_ydelayq_mul_po_kernel(
@@ -49,9 +39,9 @@ def tile_picked_ydelayq_mul_po_kernel(
         keep = ctx.enter_context(tc.tile_pool(name="keep", bufs=1))
         psum = ctx.enter_context(tc.psum_pool(name="psum", bufs=1))
 
-        offs_sb = keep.tile([P, S // 16], U16, name="offs_sb")
-        bk_sb = keep.tile([P, U // 16], U16, name="bk_sb")
-        rw_sb = keep.tile([P, U // 16], U16, name="rw_sb")
+        offs_sb = keep.tile([P, S // LIST_ROWS], U16, name="offs_sb")
+        bk_sb = keep.tile([P, U // LIST_ROWS], U16, name="bk_sb")
+        rw_sb = keep.tile([P, U // LIST_ROWS], U16, name="rw_sb")
         xw = [keep.tile([P, T], U32, name=f"xw{g}", tag=f"xw{g}", align_bytes=64) for g in range(PASSES)]
         xs = keep.tile([P, T], U8, name="xs", align_bytes=64)
         planes = keep.tile([P, PASSES, S + 2 * N], U8, name="planes", align_bytes=64)
@@ -65,8 +55,8 @@ def tile_picked_ydelayq_mul_po_kernel(
             nc.vector.memset(ws[lo:hi, :, :].bitcast(I32), 0)
         nc.vector.memset(planes[:].bitcast(I32), 0)
 
-        def load_words(queue, tile, words):
-            queue.dma_start(
+        def load_words(tile, words):
+            nc.sync.dma_start(
                 out=tile.rearrange("p (g n) -> p g n", g=words.shape[0]).bitcast(I32),
                 in_=words.rearrange("g p n -> p g n").bitcast(I32),
             )
@@ -81,50 +71,56 @@ def tile_picked_ydelayq_mul_po_kernel(
         load_rows(nc.sync, xs[0:32, :], x_scales)
         load_rows(nc.scalar, ws[0:32, 0, :], w1_scales)
         load_rows(nc.scalar, ws[0:32, 1, :], w2_scales)
-        load_words(nc.sync, w1w[:], w1_words)
+        load_words(w1w[:], w1_words)
         load_x(0)
         load_x(1)
-        load_words(nc.sync, w2w[:], w2_words)
+        load_words(w2w[:], w2_words)
         nc.sync.dma_start(bk_sb[:], bk)
         nc.sync.dma_start(rw_sb[:], rw_)
         nc.gpsimd.dma_start(out=unit_sb[:], in_=unit.rearrange("(p t) o -> p (t o)", t=PACK))
 
         xq_words = [keep.tile([P, S], U32, name=f"xq_words{g}", align_bytes=64) for g in range(PASSES)]
         xq_rows = keep.tile([P, S], U8, name="xq_rows", align_bytes=64)
-        rows = keep.tile([P, S + 2 * N], U8, name="rows", align_bytes=64)
+        scale_rows = keep.tile([P, S + 2 * N], U8, name="scale_rows", align_bytes=64)
         nc.vector.tensor_copy(
-            out=rows[:, S:].rearrange("p (w t m) -> p w t m", w=2, t=PACK), in_=ws[:].rearrange("p w (m t) -> p w t m", t=PACK)
+            out=scale_rows[:, S:].rearrange("p (w t m) -> p w t m", w=2, t=PACK), in_=ws[:].rearrange("p w (m t) -> p w t m", t=PACK)
         )
         nc.vector.tensor_copy(out=xq_rows[:], in_=xs[:].indirect(offs_sb[:]))
-        nc.vector.tensor_copy(out=rows[:, 0:S], in_=xq_rows[:])
-        for q in range(4):
-            nc.scalar.dma_start(out=planes[32 * q : 32 * q + 4, :, :].bitcast(I32), in_=rows[8 * q : 8 * q + 8, :].bitcast(I32))
+        nc.vector.tensor_copy(out=scale_rows[:, 0:S], in_=xq_rows[:])
+        for q in range(QUADRANTS):
+            nc.scalar.dma_start(out=planes[32 * q : 32 * q + 4, :, :].bitcast(I32), in_=scale_rows[8 * q : 8 * q + 8, :].bitcast(I32))
         nc.vector.tensor_copy(out=xq_words[0][:], in_=xw[0][:].indirect(offs_sb[:]))
-        w1_first = keep.tile([P, 1, 512], U8, name="w1_first", align_bytes=64)
-        deal_words(nc.scalar.copy, w1_first[:], w1w[:], 0)
+        w1_slot0 = keep.tile([P, 1, PASSES * SLOT_BYTES], U8, name="w1_slot0", align_bytes=64)
+        deal_words(nc.scalar.copy, w1_slot0[:], w1w[:], 0)
         nc.vector.tensor_copy(out=xq_words[1][:], in_=xw[1][:].indirect(offs_sb[:]))
-        w2_dealt = keep.tile([P, PACK, 512], U8, name="w2_dealt", align_bytes=64)
-        deal_words(nc.scalar.copy, w2_dealt[:], w2w[:], 0)
-        late = keep.tile([P, 3072], U8, name="late", tag="xw1", align_bytes=64)
-        w1_second = late[:, 0:1024].rearrange("p (t n) -> p t n", t=2)
-        w3_dealt = late[:, 1024:2048].rearrange("p (t n) -> p t n", t=PACK)
-        w3_planes = late[:, 2048:2560].rearrange("p (t n) -> p t n", t=PACK)
-        w1_next = late[:, 2560:3072].rearrange("p (t n) -> p t n", t=1)
-        deal_words(nc.vector.tensor_copy, w1_next, w1w[:], 1)
-        deal_words(nc.vector.tensor_copy, w1_second, w1w[:], 2)
-        w1_dealt = [w1_first[:, 0, :], w1_next[:, 0, :], w1_second[:, 0, :], w1_second[:, 1, :]]
+
+        dealt = keep.tile([P, 5120], U8, name="dealt", tag="xw1", align_bytes=64)
+        w1_slots23 = dealt[:, 0:1024].rearrange("p (t n) -> p t n", t=2)
+        w3_dealt = dealt[:, 1024:2048].rearrange("p (t n) -> p t n", t=PACK)
+        w3_planes = dealt[:, 2048:2560].rearrange("p (t n) -> p t n", t=PACK)
+        w1_slot1 = dealt[:, 2560:3072].rearrange("p (t n) -> p t n", t=1)
+        w2_dealt = dealt[:, 3072:5120].rearrange("p (t n) -> p t n", t=PACK)
+        deal_words(nc.vector.tensor_copy, w1_slot1, w1w[:], 1)
+        deal_words(nc.vector.tensor_copy, w2_dealt, w2w[:], 0)
+        deal_words(nc.vector.tensor_copy, w1_slots23, w1w[:], 2)
+        w1_dealt = [w1_slot0[:, 0, :], w1_slot1[:, 0, :], w1_slots23[:, 0, :], w1_slots23[:, 1, :]]
+
         w3w = w1w[:, 0 : 2 * N]
         w3s = w1w[:, 2 * N : 3 * N].rearrange("p (g n) -> p g n", g=1)
-        load_words(nc.sync, w3w, w3_words)
-        load_scale_rows(nc.sync, w3s, w3_scales)
+        load_words(w3w, w3_words)
+        for q in range(QUADRANTS):
+            nc.sync.dma_start(
+                out=w3s[32 * q : 32 * q + 4, :, :].bitcast(I32),
+                in_=w3_scales[:, 4 * q : 4 * q + 4, :].rearrange("g r n -> r g n").bitcast(I32),
+            )
 
         def first_product(bank, words, scale_column):
             acc = psum.tile([P, S], F32, name=f"acc{bank}", tag=f"bank{bank}")
             for g in range(PASSES):
                 nc.tensor.matmul_mx(
                     out=acc[:],
-                    lhsT=words[:, 256 * g : 256 * (g + 1)].bitcast(FP4X4),
-                    lhsT_scale=planes[:, g, scale_column : scale_column + 128],
+                    lhsT=words[:, SLOT_BYTES * g : SLOT_BYTES * (g + 1)].bitcast(FP4X4),
+                    lhsT_scale=planes[:, g, scale_column : scale_column + P],
                     rhs=xq_words[g][:].bitcast(FP8X4),
                     rhs_scale=planes[:, g, 0:S],
                     start=(g == 0),
@@ -134,14 +130,11 @@ def tile_picked_ydelayq_mul_po_kernel(
 
         y_ps = {}
         z_ps = {}
-        for t in (0, 1):
-            y_ps[t] = first_product(t, w1_dealt[t], S + 128 * t)
-        for t in (0, 1):
-            z_ps[t] = first_product(PACK + t, w2_dealt[:, t, :], S + N + 128 * t)
-        for t in (2, 3):
-            y_ps[t] = first_product(t, w1_dealt[t], S + 128 * t)
-        for t in (2, 3):
-            z_ps[t] = first_product(PACK + t, w2_dealt[:, t, :], S + N + 128 * t)
+        for pair in ((0, 1), (2, 3)):
+            for t in pair:
+                y_ps[t] = first_product(t, w1_dealt[t], S + P * t)
+            for t in pair:
+                z_ps[t] = first_product(PACK + t, w2_dealt[:, t, :], S + N + P * t)
         y = [keep.tile([P, S], F32, name=f"y{t}", align_bytes=64) for t in range(PACK)]
         z = [keep.tile([P, S], F32, name=f"z{t}", align_bytes=64) for t in range(PACK)]
 
@@ -151,80 +144,84 @@ def tile_picked_ydelayq_mul_po_kernel(
         starts = [sum(CHUNKS[:c]) for c in range(len(CHUNKS))]
 
         def per_chunk(name, dtype, shape):
-            return [keep.tile(shape(n), dtype, name=f"{name}{c}", align_bytes=64) for c, n in enumerate(CHUNKS)]
+            return [keep.tile(shape(n), dtype, name=f"{name}{c}", tag=f"{name}{c}", align_bytes=64) for c, n in enumerate(CHUNKS)]
 
-        yk = per_chunk("yk", F32, lambda n: [P, PACK, n])
-        yr = per_chunk("yr", F32, lambda n: [P, PACK, n])
-        busy = per_chunk("busy", F32, lambda n: [P, PACK, n])
+        spans = (CHUNKS[0], CHUNKS[1], CHUNKS[2] + CHUNKS[3])
+
+        def per_span(name):
+            return [keep.tile([P, PACK, n], F32, name=f"{name}{s}", align_bytes=64) for s, n in enumerate(spans)]
+
+        yk = per_span("yk")
+        yr = per_span("yr")
+        busy_span = per_span("busy")
+        busy = [busy_span[0][:], busy_span[1][:], busy_span[2][:, :, 0 : CHUNKS[2]], busy_span[2][:, :, CHUNKS[2] :]]
         prod = per_chunk("prod", F32, lambda n: [P, PACK, n])
         hid = per_chunk("hid", F32, lambda n: [P, PACK, n])
         hid_bf = per_chunk("hid_bf", BF16, lambda n: [P, n, PACK])
         hid_codes = per_chunk("hid_codes", U32, lambda n: [P, n])
         hid_scales = per_chunk("hid_scales", U8, lambda n: [P, n])
         out_sb = per_chunk("out_sb", F32, lambda n: [P, PACK, n])
-        out_bf = per_chunk("out_bf", BF16, lambda n: [P, n, PACK])
-        out_codes = per_chunk("out_codes", U32, lambda n: [P, n])
+        out_bf = {}
         zk = {c: keep.tile([P, PACK, CHUNKS[c]], F32, name=f"zk{c}", align_bytes=64) for c in (3,)}
         zr = {c: keep.tile([P, PACK, CHUNKS[c]], F32, name=f"zr{c}", align_bytes=64) for c in (2, 3)}
         out_ps = {}
 
-        def entries(lst, c):
-            return lst[:, starts[c] // 16 : (starts[c] + CHUNKS[c]) // 16]
+        taken_over = {("out_bf", 1): "hid3", ("out_bf", 2): "hid_bf3", ("out_codes", 1): "hid_codes3"}
 
-        def y_out(t):
+        def plane_tile(name, c, dtype, shape):
+            tag = taken_over.get((name, c), f"{name}{c}")
+            return keep.tile(shape, dtype, name=f"{name}{c}", tag=tag, align_bytes=64)
+
+        def chunk_entries(lst, c):
+            return lst[:, starts[c] // LIST_ROWS : (starts[c] + CHUNKS[c]) // LIST_ROWS]
+
+        def span_entries(lst, s):
+            return lst[:, starts[s] // LIST_ROWS : (starts[s] + spans[s]) // LIST_ROWS]
+
+        def y_window(t):
             nc.scalar.activation(out=y[t][:], in_=y_ps[t][:], func=COPY)
 
-        def z_out_scalar(t):
+        def z_window_scalar(t):
             nc.scalar.activation(out=z[t][:], in_=z_ps[t][:], func=COPY, scale=unit_sb[:, t : t + 1])
 
-        def z_out_vector(t):
+        def z_window_vector(t):
             nc.vector.tensor_scalar(out=z[t][:], in0=z_ps[t][:], scalar1=unit_sb[:, t : t + 1], scalar2=None, op0=ALU.mult)
 
-        def fetch_k(c, t):
-            nc.scalar.activation(out=yk[c][:, t, :], in_=y[t][:].indirect(entries(bk_sb, c)), func=COPY)
+        def fetch_yk(s, t):
+            nc.scalar.activation(out=yk[s][:, t, :], in_=y[t][:].indirect(span_entries(bk_sb, s)), func=COPY)
 
-        def fetch_r(c, t):
-            nc.scalar.activation(out=yr[c][:, t, :], in_=y[t][:].indirect(entries(rw_sb, c)), func=COPY)
+        def fetch_y(s, slots):
+            for t in slots:
+                fetch_yk(s, t)
+                nc.scalar.activation(out=yr[s][:, t, :], in_=y[t][:].indirect(span_entries(rw_sb, s)), func=COPY)
 
-        def fetch_r_vector(c, t):
-            nc.vector.tensor_copy(out=yr[c][:, t, :], in_=y[t][:].indirect(entries(rw_sb, c)))
-
-        def fetch_zk(c):
+        def fetch_z(fetched, lst, c):
             for t in range(PACK):
-                nc.scalar.activation(out=zk[c][:, t, :], in_=z[t][:].indirect(entries(bk_sb, c)), func=COPY)
+                nc.scalar.activation(out=fetched[c][:, t, :], in_=z[t][:].indirect(chunk_entries(lst, c)), func=COPY)
 
-        def fetch_zr(c):
-            for t in range(PACK):
-                nc.scalar.activation(out=zr[c][:, t, :], in_=z[t][:].indirect(entries(rw_sb, c)), func=COPY)
+        def larger(s, t0, t1):
+            nc.vector.tensor_tensor(out=busy_span[s][:, t0:t1, :], in0=yk[s][:, t0:t1, :], in1=yr[s][:, t0:t1, :], op=ALU.max)
+
+        def times_zk(c, t):
+            nc.vector.tensor_tensor(out=prod[c][:, t, :], in0=z[t][:].indirect(chunk_entries(bk_sb, c)), in1=busy[c][:, t, :], op=ALU.mult)
+
+        def plus_zr(c, t):
+            nc.vector.tensor_tensor(out=hid[c][:, t, :], in0=z[t][:].indirect(chunk_entries(rw_sb, c)), in1=prod[c][:, t, :], op=ALU.add)
 
         def times_fetched(c):
-            nc.vector.tensor_tensor(out=prod[c][:], in0=zk[c][:], in1=busy[c][:], op=ALU.mult)
+            nc.vector.tensor_tensor(out=prod[c][:], in0=zk[c][:], in1=busy[c], op=ALU.mult)
 
         def plus_fetched(c):
             nc.vector.tensor_tensor(out=hid[c][:], in0=zr[c][:], in1=prod[c][:], op=ALU.add)
 
-        def fetch(c, ts):
-            for t in ts:
-                fetch_k(c, t)
-                fetch_r(c, t)
-
-        def later(c, t0, t1):
-            nc.vector.tensor_tensor(out=busy[c][:, t0:t1, :], in0=yk[c][:, t0:t1, :], in1=yr[c][:, t0:t1, :], op=ALU.max)
-
-        def times(c, t):
-            nc.vector.tensor_tensor(out=prod[c][:, t, :], in0=z[t][:].indirect(entries(bk_sb, c)), in1=busy[c][:, t, :], op=ALU.mult)
-
-        def plus(c, t):
-            nc.vector.tensor_tensor(out=hid[c][:, t, :], in0=z[t][:].indirect(entries(rw_sb, c)), in1=prod[c][:, t, :], op=ALU.add)
-
-        def interleave(dst, src):
+        def round_slots(dst, src):
             nc.vector.tensor_copy(
-                out=dst.rearrange("p (c i) t -> p c t i", i=4),
-                in_=src.rearrange("p t (c i) -> p c t i", i=4),
+                out=dst.rearrange("p (c i) t -> p c t i", i=LINE),
+                in_=src.rearrange("p t (c i) -> p c t i", i=LINE),
             )
 
         def round_hid(c):
-            interleave(hid_bf[c][:], hid[c][:])
+            round_slots(hid_bf[c][:], hid[c][:])
 
         def last_product(c):
             nc.vector.quantize_mx(out=hid_codes[c][:].bitcast(FP8X4), scales=hid_scales[c][:], in_=hid_bf[c][:].rearrange("p r t -> p (r t)"))
@@ -248,8 +245,10 @@ def tile_picked_ydelayq_mul_po_kernel(
             n = CHUNKS[c]
             for b in range(n // BLOCK):
                 nc.scalar.activation(out=out_sb[c][:, :, b * BLOCK : (b + 1) * BLOCK], in_=out_ps[(c, b)][:], func=COPY)
-            queue = nc.scalar if c == len(CHUNKS) - 1 else nc.sync
-            queue.dma_start(out=out_rows[:, :, starts[c] : starts[c] + n], in_=out_sb[c][:])
+            nc.sync.dma_start(out=out_rows[:, :, starts[c] : starts[c] + n], in_=out_sb[c][:])
+
+        def open_out_bf(c):
+            out_bf[c] = plane_tile("out_bf", c, BF16, [P, CHUNKS[c], PACK])
 
         def round_out_scalar(c, blocks):
             for b in blocks:
@@ -259,90 +258,94 @@ def tile_picked_ydelayq_mul_po_kernel(
 
         def round_out_vector(c, b):
             cols = slice(b * BLOCK, (b + 1) * BLOCK)
-            interleave(out_bf[c][:, cols, :], out_sb[c][:, :, cols])
+            round_slots(out_bf[c][:, cols, :], out_sb[c][:, :, cols])
 
-        def round_out_vector_psum(c):
-            nc.vector.tensor_copy(out=out_bf[c][:], in_=out_ps[(c, 0)][:].rearrange("p t r -> p r t"))
-
-        def store_planes(c):
+        def store_codes(c):
             cols = slice(starts[c], starts[c] + CHUNKS[c])
-            nc.vector.quantize_mx(out=out_codes[c][:].bitcast(FP8X4), scales=out_scales[:, cols], in_=out_bf[c][:].rearrange("p r t -> p (r t)"))
-            nc.sync.dma_start(out=out_words[:, cols], in_=out_codes[c][:].bitcast(I32))
+            codes = plane_tile("out_codes", c, U32, [P, CHUNKS[c]])
+            nc.vector.quantize_mx(out=codes[:].bitcast(FP8X4), scales=out_scales[:, cols], in_=out_bf[c][:].rearrange("p r t -> p (r t)"))
+            nc.sync.dma_start(out=out_words[:, cols], in_=codes[:].bitcast(I32))
 
-        y_out(0)
-        y_out(1)
-        fetch_k(0, 0)
-        fetch_r_vector(0, 0)
-        fetch(0, [1])
-        z_out_vector(0)
-        later(0, 0, 1)
-        z_out_vector(1)
-        y_out(2)
-        y_out(3)
-        fetch(0, [2])
-        z_out_scalar(3)
-        fetch(0, [3])
-        times(0, 0)
-        later(0, 1, 2)
-        plus(0, 0)
-        times(0, 1)
-        z_out_vector(2)
-        plus(0, 1)
-        later(0, 2, 3)
+
+        y_window(0)
+        y_window(1)
+        fetch_yk(0, 0)
+        nc.vector.tensor_copy(out=yr[0][:, 0, :], in_=y[0][:].indirect(span_entries(rw_sb, 0)))
+        fetch_y(0, [1])
+        z_window_vector(0)
+        larger(0, 0, 1)
+        z_window_vector(1)
+        y_window(2)
+        y_window(3)
+        fetch_y(0, [2])
+        z_window_scalar(3)
+        fetch_y(0, [3])
+        times_zk(0, 0)
+        larger(0, 1, 2)
+        plus_zr(0, 0)
+        times_zk(0, 1)
+        z_window_vector(2)
+        plus_zr(0, 1)
+        larger(0, 2, 3)
         deal_words(nc.vector.tensor_copy, w3_dealt, w3w, 0)
-        times(0, 2)
-        later(0, 3, 4)
-        plus(0, 2)
-        times(0, 3)
-        deal_scales(nc.vector.tensor_copy, w3_planes, w3s, 0)
-        plus(0, 3)
-        fetch(1, [0, 1])
-        later(1, 0, 2)
+        times_zk(0, 2)
+        larger(0, 3, 4)
+        plus_zr(0, 2)
+        times_zk(0, 3)
+        nc.vector.tensor_copy(out=w3_planes, in_=w3s.rearrange("p g (m t) -> p t (g m)", t=PACK))
+        plus_zr(0, 3)
+
+        fetch_y(1, [0, 1])
+        larger(1, 0, 2)
         round_hid(0)
-        times(1, 0)
+        times_zk(1, 0)
         last_product(0)
-        times(1, 1)
-        fetch(1, [2, 3])
-        later(1, 2, 4)
-        plus(1, 0)
-        plus(1, 1)
-        fetch(2, [0, 1, 2, 3])
+        times_zk(1, 1)
+        fetch_y(1, [2, 3])
+        larger(1, 2, 4)
+        plus_zr(1, 0)
+        plus_zr(1, 1)
+        fetch_y(2, range(PACK))
         store_values(0)
-        fetch_zr(2)
-        round_out_scalar(0, (0, 1, 2))
-        fetch(3, [0, 1, 2, 3])
-        fetch_zk(3)
-        fetch_zr(3)
-        times(1, 2)
-        times(1, 3)
-        later(2, 0, 4)
-        plus(1, 2)
-        plus(1, 3)
-        times(2, 0)
+        fetch_z(zr, rw_sb, 2)
+        open_out_bf(0)
+        round_out_scalar(0, range(CHUNKS[0] // BLOCK))
+        fetch_z(zk, bk_sb, 3)
+        fetch_z(zr, rw_sb, 3)
+        times_zk(1, 2)
+        times_zk(1, 3)
+        larger(2, 0, PACK)
+        plus_zr(1, 2)
+        plus_zr(1, 3)
+
+        times_zk(2, 0)
         round_hid(1)
-        times(2, 1)
+        times_zk(2, 1)
         last_product(1)
-        times(2, 2)
-        times(2, 3)
-        store_planes(0)
+        times_zk(2, 2)
+        times_zk(2, 3)
+        store_codes(0)
         plus_fetched(2)
         store_values(1)
-        later(3, 0, 4)
-        round_hid(2)
         times_fetched(3)
-        last_product(2)
+        round_hid(2)
         plus_fetched(3)
+        last_product(2)
         round_hid(3)
         store_values(2)
+
+        open_out_bf(1)
+        round_out_vector(1, 2)
         round_out_scalar(1, (0, 1))
         last_product(3)
+        open_out_bf(2)
         round_out_vector(2, 0)
-        round_out_vector(1, 2)
-        store_planes(2)
-        round_out_vector_psum(3)
+        store_codes(2)
+        open_out_bf(3)
+        nc.vector.tensor_copy(out=out_bf[3][:], in_=out_ps[(3, 0)][:].rearrange("p t r -> p r t"))
         store_values(3)
-        store_planes(1)
-        store_planes(3)
-        for q in range(4):
+        store_codes(1)
+        store_codes(3)
+        for q in range(QUADRANTS):
             queue = nc.sync if q % 2 == 0 else nc.scalar
             queue.dma_start(out=out_2[0, 4 * q : 4 * q + 4, :].bitcast(I32), in_=out_scales[32 * q : 32 * q + 4, :].bitcast(I32))

from contextlib import ExitStack

import concourse.mybir as mybir

K, T, S, N, H, U = 1024, 2048, 512, 512, 512, 1024
FLOPS = 2 * K * N * S * 2 + 2 * H * N * U

F32 = mybir.dt.float32
BF16 = mybir.dt.bfloat16
I32 = mybir.dt.int32
U32 = mybir.dt.uint32
U16 = mybir.dt.uint16
U8 = mybir.dt.uint8
FP8X4 = mybir.dt.float8_e4m3fn_x4
FP4X4 = mybir.dt.float4_e2m1fn_x4
ALU = mybir.AluOpType
COPY = mybir.ActivationFunctionType.Copy

P = 128
PACK = 4
PASSES = K // (P * PACK)
QUADRANTS = 4
LIST_ROWS = 16
SLOT_BYTES = 2 * P
BLOCK = 128
LINE = 4
CHUNKS = (384, 384, 128, 128)


def deal_words(copy, dealt, words, t0):
    copy(out=dealt.bitcast(U16), in_=words.bitcast(U16).rearrange("p (m t) -> p t m", t=PACK)[:, t0 : t0 + dealt.shape[1], :])


def tile_picked_ydelayq_mul_po_kernel(
    tc, x_words, x_scales, w1_words, w1_scales, w2_words, w2_scales, unit, w3_words, w3_scales, offs, bk, rw_, out_0, out_1, out_2
):
    nc = tc.nc
    with ExitStack() as ctx:
        keep = ctx.enter_context(tc.tile_pool(name="keep", bufs=1))
        psum = ctx.enter_context(tc.psum_pool(name="psum", bufs=1))

        offs_sb = keep.tile([P, S // LIST_ROWS], U16, name="offs_sb")
        bk_sb = keep.tile([P, U // LIST_ROWS], U16, name="bk_sb")
        rw_sb = keep.tile([P, U // LIST_ROWS], U16, name="rw_sb")
        xw = [keep.tile([P, T], U32, name=f"xw{g}", tag=f"xw{g}", align_bytes=64) for g in range(PASSES)]
        xs = keep.tile([P, T], U8, name="xs", align_bytes=64)
        planes = keep.tile([P, PASSES, S + 2 * N], U8, name="planes", align_bytes=64)
        w1w = keep.tile([P, PASSES * 2 * N], U8, name="w1w", align_bytes=64)
        w2w = keep.tile([P, PASSES * 2 * N], U8, name="w2w", align_bytes=64)
        ws = keep.tile([P, 2, N], U8, name="ws", align_bytes=64)
        unit_sb = keep.tile([P, PACK], F32, name="unit_sb")

        for lo, hi in ((32, 64), (64, 128)):
            nc.vector.memset(xs[lo:hi, :].bitcast(I32), 0)
            nc.vector.memset(ws[lo:hi, :, :].bitcast(I32), 0)
        nc.vector.memset(planes[:].bitcast(I32), 0)

        def load_words(tile, words):
            nc.sync.dma_start(
                out=tile.rearrange("p (g n) -> p g n", g=words.shape[0]).bitcast(I32),
                in_=words.rearrange("g p n -> p g n").bitcast(I32),
            )

        def load_x(g):
            nc.sync.dma_start(out=xw[g][:].bitcast(I32), in_=x_words[g].rearrange("p n t -> p (n t)").bitcast(I32))

        def load_rows(queue, rows, scales):
            queue.dma_start(out=rows.bitcast(I32), in_=scales.rearrange("g r n -> r g n").bitcast(I32))

        nc.sync.dma_start(offs_sb[:], offs)
        load_rows(nc.sync, xs[0:32, :], x_scales)
        load_rows(nc.scalar, ws[0:32, 0, :], w1_scales)
        load_rows(nc.scalar, ws[0:32, 1, :], w2_scales)
        load_words(w1w[:], w1_words)
        load_x(0)
        load_x(1)
        load_words(w2w[:], w2_words)
        nc.sync.dma_start(bk_sb[:], bk)
        nc.sync.dma_start(rw_sb[:], rw_)
        nc.gpsimd.dma_start(out=unit_sb[:], in_=unit.rearrange("(p t) o -> p (t o)", t=PACK))

        xq_words = [keep.tile([P, S], U32, name=f"xq_words{g}", align_bytes=64) for g in range(PASSES)]
        xq_rows = keep.tile([P, S], U8, name="xq_rows", align_bytes=64)
        scale_rows = keep.tile([P, S + 2 * N], U8, name="scale_rows", align_bytes=64)
        nc.vector.tensor_copy(
            out=scale_rows[:, S:].rearrange("p (w t m) -> p w t m", w=2, t=PACK), in_=ws[:].rearrange("p w (m t) -> p w t m", t=PACK)
        )
        nc.vector.tensor_copy(out=xq_rows[:], in_=xs[:].indirect(offs_sb[:]))
        nc.vector.tensor_copy(out=scale_rows[:, 0:S], in_=xq_rows[:])
        for q in range(QUADRANTS):
            nc.scalar.dma_start(out=planes[32 * q : 32 * q + 4, :, :].bitcast(I32), in_=scale_rows[8 * q : 8 * q + 8, :].bitcast(I32))
        nc.vector.tensor_copy(out=xq_words[0][:], in_=xw[0][:].indirect(offs_sb[:]))
        w1_slot0 = keep.tile([P, 1, PASSES * SLOT_BYTES], U8, name="w1_slot0", align_bytes=64)
        deal_words(nc.scalar.copy, w1_slot0[:], w1w[:], 0)
        nc.vector.tensor_copy(out=xq_words[1][:], in_=xw[1][:].indirect(offs_sb[:]))

        dealt = keep.tile([P, 5120], U8, name="dealt", tag="xw1", align_bytes=64)
        w1_slots23 = dealt[:, 0:1024].rearrange("p (t n) -> p t n", t=2)
        w3_dealt = dealt[:, 1024:2048].rearrange("p (t n) -> p t n", t=PACK)
        w3_planes = dealt[:, 2048:2560].rearrange("p (t n) -> p t n", t=PACK)
        w1_slot1 = dealt[:, 2560:3072].rearrange("p (t n) -> p t n", t=1)
        w2_dealt = dealt[:, 3072:5120].rearrange("p (t n) -> p t n", t=PACK)
        deal_words(nc.vector.tensor_copy, w1_slot1, w1w[:], 1)
        deal_words(nc.vector.tensor_copy, w2_dealt, w2w[:], 0)
        deal_words(nc.vector.tensor_copy, w1_slots23, w1w[:], 2)
        w1_dealt = [w1_slot0[:, 0, :], w1_slot1[:, 0, :], w1_slots23[:, 0, :], w1_slots23[:, 1, :]]

        w3w = w1w[:, 0 : 2 * N]
        w3s = w1w[:, 2 * N : 3 * N].rearrange("p (g n) -> p g n", g=1)
        load_words(w3w, w3_words)
        for q in range(QUADRANTS):
            nc.sync.dma_start(
                out=w3s[32 * q : 32 * q + 4, :, :].bitcast(I32),
                in_=w3_scales[:, 4 * q : 4 * q + 4, :].rearrange("g r n -> r g n").bitcast(I32),
            )

        def first_product(bank, words, scale_column):
            acc = psum.tile([P, S], F32, name=f"acc{bank}", tag=f"bank{bank}")
            for g in range(PASSES):
                nc.tensor.matmul_mx(
                    out=acc[:],
                    lhsT=words[:, SLOT_BYTES * g : SLOT_BYTES * (g + 1)].bitcast(FP4X4),
                    lhsT_scale=planes[:, g, scale_column : scale_column + P],
                    rhs=xq_words[g][:].bitcast(FP8X4),
                    rhs_scale=planes[:, g, 0:S],
                    start=(g == 0),
                    stop=(g == PASSES - 1),
                )
            return acc

        y_ps = {}
        z_ps = {}
        for pair in ((0, 1), (2, 3)):
            for t in pair:
                y_ps[t] = first_product(t, w1_dealt[t], S + P * t)
            for t in pair:
                z_ps[t] = first_product(PACK + t, w2_dealt[:, t, :], S + N + P * t)
        y = [keep.tile([P, S], F32, name=f"y{t}", align_bytes=64) for t in range(PACK)]
        z = [keep.tile([P, S], F32, name=f"z{t}", align_bytes=64) for t in range(PACK)]

        out_scales = keep.tile([P, U], U8, name="out_scales", align_bytes=64)
        out_rows = out_0.rearrange("(p t) r -> p t r", t=PACK)
        out_words = out_1[0].rearrange("p r t -> p (r t)").bitcast(I32)
        starts = [sum(CHUNKS[:c]) for c in range(len(CHUNKS))]

        def per_chunk(name, dtype, shape):
            return [keep.tile(shape(n), dtype, name=f"{name}{c}", tag=f"{name}{c}", align_bytes=64) for c, n in enumerate(CHUNKS)]

        spans = (CHUNKS[0], CHUNKS[1], CHUNKS[2] + CHUNKS[3])

        def per_span(name):
            return [keep.tile([P, PACK, n], F32, name=f"{name}{s}", align_bytes=64) for s, n in enumerate(spans)]

        yk = per_span("yk")
        yr = per_span("yr")
        busy_span = per_span("busy")
        busy = [busy_span[0][:], busy_span[1][:], busy_span[2][:, :, 0 : CHUNKS[2]], busy_span[2][:, :, CHUNKS[2] :]]
        prod = per_chunk("prod", F32, lambda n: [P, PACK, n])
        hid = per_chunk("hid", F32, lambda n: [P, PACK, n])
        hid_bf = per_chunk("hid_bf", BF16, lambda n: [P, n, PACK])
        hid_codes = per_chunk("hid_codes", U32, lambda n: [P, n])
        hid_scales = per_chunk("hid_scales", U8, lambda n: [P, n])
        out_sb = per_chunk("out_sb", F32, lambda n: [P, PACK, n])
        out_bf = {}
        zk = {c: keep.tile([P, PACK, CHUNKS[c]], F32, name=f"zk{c}", align_bytes=64) for c in (3,)}
        zr = {c: keep.tile([P, PACK, CHUNKS[c]], F32, name=f"zr{c}", align_bytes=64) for c in (2, 3)}
        out_ps = {}

        taken_over = {("out_bf", 1): "hid3", ("out_bf", 2): "hid_bf3", ("out_codes", 1): "hid_codes3"}

        def plane_tile(name, c, dtype, shape):
            tag = taken_over.get((name, c), f"{name}{c}")
            return keep.tile(shape, dtype, name=f"{name}{c}", tag=tag, align_bytes=64)

        def chunk_entries(lst, c):
            return lst[:, starts[c] // LIST_ROWS : (starts[c] + CHUNKS[c]) // LIST_ROWS]

        def span_entries(lst, s):
            return lst[:, starts[s] // LIST_ROWS : (starts[s] + spans[s]) // LIST_ROWS]

        def y_window(t):
            nc.scalar.activation(out=y[t][:], in_=y_ps[t][:], func=COPY)

        def z_window_scalar(t):
            nc.scalar.activation(out=z[t][:], in_=z_ps[t][:], func=COPY, scale=unit_sb[:, t : t + 1])

        def z_window_vector(t):
            nc.vector.tensor_scalar(out=z[t][:], in0=z_ps[t][:], scalar1=unit_sb[:, t : t + 1], scalar2=None, op0=ALU.mult)

        def fetch_yk(s, t):
            nc.scalar.activation(out=yk[s][:, t, :], in_=y[t][:].indirect(span_entries(bk_sb, s)), func=COPY)

        def fetch_y(s, slots):
            for t in slots:
                fetch_yk(s, t)
                nc.scalar.activation(out=yr[s][:, t, :], in_=y[t][:].indirect(span_entries(rw_sb, s)), func=COPY)

        def fetch_z(fetched, lst, c):
            for t in range(PACK):
                nc.scalar.activation(out=fetched[c][:, t, :], in_=z[t][:].indirect(chunk_entries(lst, c)), func=COPY)

        def larger(s, t0, t1):
            nc.vector.tensor_tensor(out=busy_span[s][:, t0:t1, :], in0=yk[s][:, t0:t1, :], in1=yr[s][:, t0:t1, :], op=ALU.max)

        def times_zk(c, t):
            nc.vector.tensor_tensor(out=prod[c][:, t, :], in0=z[t][:].indirect(chunk_entries(bk_sb, c)), in1=busy[c][:, t, :], op=ALU.mult)

        def plus_zr(c, t):
            nc.vector.tensor_tensor(out=hid[c][:, t, :], in0=z[t][:].indirect(chunk_entries(rw_sb, c)), in1=prod[c][:, t, :], op=ALU.add)

        def times_fetched(c):
            nc.vector.tensor_tensor(out=prod[c][:], in0=zk[c][:], in1=busy[c], op=ALU.mult)

        def plus_fetched(c):
            nc.vector.tensor_tensor(out=hid[c][:], in0=zr[c][:], in1=prod[c][:], op=ALU.add)

        def round_slots(dst, src):
            nc.vector.tensor_copy(
                out=dst.rearrange("p (c i) t -> p c t i", i=LINE),
                in_=src.rearrange("p t (c i) -> p c t i", i=LINE),
            )

        def round_hid(c):
            round_slots(hid_bf[c][:], hid[c][:])

        def last_product(c):
            nc.vector.quantize_mx(out=hid_codes[c][:].bitcast(FP8X4), scales=hid_scales[c][:], in_=hid_bf[c][:].rearrange("p r t -> p (r t)"))
            for b in range(CHUNKS[c] // BLOCK):
                bank = starts[c] // BLOCK + b
                acc = psum.tile([P, PACK, BLOCK], F32, name=f"out_ps{bank}", tag=f"bank{bank}")
                cols = slice(b * BLOCK, (b + 1) * BLOCK)
                for t in range(PACK):
                    nc.tensor.matmul_mx(
                        out=acc[:, t, :],
                        lhsT=w3_dealt[:, t, :].bitcast(FP4X4),
                        lhsT_scale=w3_planes[:, t, :],
                        rhs=hid_codes[c][:, cols].bitcast(FP8X4),
                        rhs_scale=hid_scales[c][:, cols],
                        start=True,
                        stop=True,
                    )
                out_ps[(c, b)] = acc

        def store_values(c):
            n = CHUNKS[c]
            for b in range(n // BLOCK):
                nc.scalar.activation(out=out_sb[c][:, :, b * BLOCK : (b + 1) * BLOCK], in_=out_ps[(c, b)][:], func=COPY)
            nc.sync.dma_start(out=out_rows[:, :, starts[c] : starts[c] + n], in_=out_sb[c][:])

        def open_out_bf(c):
            out_bf[c] = plane_tile("out_bf", c, BF16, [P, CHUNKS[c], PACK])

        def round_out_scalar(c, blocks):
            for b in blocks:
                nc.scalar.activation(
                    out=out_bf[c][:, b * BLOCK : (b + 1) * BLOCK, :], in_=out_ps[(c, b)][:].rearrange("p t r -> p r t"), func=COPY
                )

        def round_out_vector(c, b):
            cols = slice(b * BLOCK, (b + 1) * BLOCK)
            round_slots(out_bf[c][:, cols, :], out_sb[c][:, :, cols])

        def store_codes(c):
            cols = slice(starts[c], starts[c] + CHUNKS[c])
            codes = plane_tile("out_codes", c, U32, [P, CHUNKS[c]])
            nc.vector.quantize_mx(out=codes[:].bitcast(FP8X4), scales=out_scales[:, cols], in_=out_bf[c][:].rearrange("p r t -> p (r t)"))
            nc.sync.dma_start(out=out_words[:, cols], in_=codes[:].bitcast(I32))


        y_window(0)
        y_window(1)
        fetch_yk(0, 0)
        nc.vector.tensor_copy(out=yr[0][:, 0, :], in_=y[0][:].indirect(span_entries(rw_sb, 0)))
        fetch_y(0, [1])
        z_window_vector(0)
        larger(0, 0, 1)
        z_window_vector(1)
        y_window(2)
        y_window(3)
        fetch_y(0, [2])
        z_window_scalar(3)
        fetch_y(0, [3])
        times_zk(0, 0)
        larger(0, 1, 2)
        plus_zr(0, 0)
        times_zk(0, 1)
        z_window_vector(2)
        plus_zr(0, 1)
        larger(0, 2, 3)
        deal_words(nc.vector.tensor_copy, w3_dealt, w3w, 0)
        times_zk(0, 2)
        larger(0, 3, 4)
        plus_zr(0, 2)
        times_zk(0, 3)
        nc.vector.tensor_copy(out=w3_planes, in_=w3s.rearrange("p g (m t) -> p t (g m)", t=PACK))
        plus_zr(0, 3)

        fetch_y(1, [0, 1])
        larger(1, 0, 2)
        round_hid(0)
        times_zk(1, 0)
        last_product(0)
        times_zk(1, 1)
        fetch_y(1, [2, 3])
        larger(1, 2, 4)
        plus_zr(1, 0)
        plus_zr(1, 1)
        fetch_y(2, range(PACK))
        store_values(0)
        fetch_z(zr, rw_sb, 2)
        open_out_bf(0)
        round_out_scalar(0, range(CHUNKS[0] // BLOCK))
        fetch_z(zk, bk_sb, 3)
        fetch_z(zr, rw_sb, 3)
        times_zk(1, 2)
        times_zk(1, 3)
        larger(2, 0, PACK)
        plus_zr(1, 2)
        plus_zr(1, 3)

        times_zk(2, 0)
        round_hid(1)
        times_zk(2, 1)
        last_product(1)
        times_zk(2, 2)
        times_zk(2, 3)
        store_codes(0)
        plus_fetched(2)
        store_values(1)
        times_fetched(3)
        round_hid(2)
        plus_fetched(3)
        last_product(2)
        round_hid(3)
        store_values(2)

        open_out_bf(1)
        round_out_vector(1, 2)
        round_out_scalar(1, (0, 1))
        last_product(3)
        open_out_bf(2)
        round_out_vector(2, 0)
        store_codes(2)
        open_out_bf(3)
        nc.vector.tensor_copy(out=out_bf[3][:], in_=out_ps[(3, 0)][:].rearrange("p t r -> p r t"))
        store_values(3)
        store_codes(1)
        store_codes(3)
        for q in range(QUADRANTS):
            queue = nc.sync if q % 2 == 0 else nc.scalar
            queue.dma_start(out=out_2[0, 4 * q : 4 * q + 4, :].bitcast(I32), in_=out_scales[32 * q : 32 * q + 4, :].bitcast(I32))
